import numpy as np
import ml_dtypes


def mxq(x, axis, fmt="e4m3"):
    dtype, down = {"e4m3": (ml_dtypes.float8_e4m3fn, 7), "e5m2": (ml_dtypes.float8_e5m2, 14)}[fmt]
    v = np.moveaxis(np.asarray(x, np.float32).astype(ml_dtypes.bfloat16).astype(np.float64), axis, -1)
    blocks = v.reshape(v.shape[:-1] + (-1, 32))
    amax = np.abs(blocks).max(-1, keepdims=True)
    byte = np.maximum(np.where(amax > 0, np.frexp(amax)[1] - 1 + 127, 0) - down, 1)
    scale = np.exp2(byte - 127.0)
    codes = (blocks / scale).astype(np.float32).astype(dtype).astype(np.float64)
    return np.moveaxis((codes * scale).reshape(v.shape), -1, axis)


WIDE = False


def mx_kscale(k):
    if not WIDE:
        return np.ones(k)
    levels = np.array([10, -10, 5, -5, 0])
    if k % 512:
        return np.exp2(np.random.permutation(np.resize(levels, k // 32))).repeat(32)
    a = np.empty((k // 512, 16))
    for p in range(k // 512):
        a[p, :8] = np.random.permutation(np.resize(levels, 8))
        for g in range(8):
            far = levels[np.abs(levels - a[p, g]) >= 10]
            a[p, g + 8] = far[np.random.randint(len(far))]
    return np.exp2(a.ravel()).repeat(32)


def f64(x):
    return np.asarray(x).astype(np.float64)


def striped(idx):
    return np.tile(idx.reshape(-1, 16).T, (8, 1)).astype(np.uint16)


def unstriped(offs):
    return offs[:16].T.reshape(-1).astype(np.int64)


E2M1 = np.array([0.0, 0.5, 1.0, 1.5, 2.0, 3.0, 4.0, 6.0, -0.0, -0.5, -1.0, -1.5, -2.0, -3.0, -4.0, -6.0])


def pack_weight(w, fmt):
    k, n = w.shape
    w = f64(np.asarray(w, np.float32).astype(ml_dtypes.bfloat16)).reshape(k // 32, 32, n)
    amax = np.abs(w).max(1)
    if fmt == "e4m3":
        byte = np.frexp(amax)[1] - 1 + 127 - 7
    else:
        mant, ex = np.frexp(amax / 6.0)
        byte = np.where(mant > 0.5, ex, ex - 1) + 127
    byte = np.clip(np.where(amax > 0, byte, 1), 1, 254)
    scaled = (w * np.exp2(127.0 - byte)[:, None, :]).reshape(k, n).astype(np.float32)
    by_word = np.ascontiguousarray(scaled.reshape(k // 512, 128, 4, n).transpose(0, 1, 3, 2))
    if fmt == "e4m3":
        words = by_word.astype(ml_dtypes.float8_e4m3fn).view(np.uint8)
    else:
        c = by_word.astype(ml_dtypes.float4_e2m1fn).view(np.uint8) & 0xF
        words = (c[..., 0::2] | (c[..., 1::2] << 4)).reshape(k // 512, 128, 2 * n)
    return np.ascontiguousarray(words), np.ascontiguousarray(byte.astype(np.uint8).reshape(k // 512, 16, n))


def unpack_weight(words, scales, fmt):
    g, _, n = scales.shape
    words = np.ascontiguousarray(words).reshape(g, 128, n, -1)
    if fmt == "e4m3":
        vals = words.view(ml_dtypes.float8_e4m3fn).astype(np.float64)
    else:
        nib = np.empty((g, 128, n, 4), np.uint8)
        nib[..., 0::2] = words & 0xF
        nib[..., 1::2] = words >> 4
        vals = E2M1[nib]
    vals = vals * np.repeat(np.exp2(scales.astype(np.float64) - 127.0), 8, axis=1)[..., None]
    return vals.transpose(0, 1, 3, 2).reshape(g * 512, n)


def gelu(v):
    return 0.5 * v * (1.0 + np.tanh(np.sqrt(2.0 / np.pi) * (v + 0.044715 * v**3)))


K, H, N, T, S = 2048, 512, 512, 4096, 1024

def setup_inputs():
    n = np.random.standard_normal
    s = mx_kscale(K)[:, None]
    u = mx_kscale(H)[:, None]
    tab_words, tab_scales = pack_weight(n((K, T)) * np.exp(0.3 * n((1, T))) * s, "e4m3")
    w1 = (n((K, H)) / np.sqrt(K) / s).astype(np.float32)
    w4_words, w4_scales = pack_weight(n((K, H)) / np.sqrt(K) / s, "e2m1")
    c = (0.7 * n(H)).astype(np.float32)
    gain = (np.exp(0.3 * n(H)) * u[:, 0]).astype(np.float32)
    wm = (np.square(n((H, N))) / H / u).astype(np.float32)
    offs = striped(np.random.permutation(T)[:S])
    return {"tab_words": tab_words, "tab_scales": tab_scales, "offs": offs, "w1": w1,
            "w4_words": w4_words, "w4_scales": w4_scales, "c": c, "gain": gain, "wm": wm}

def reference(tab_words, tab_scales, offs, w1, w4_words, w4_scales, c, gain, wm):
    v = unpack_weight(tab_words, tab_scales, "e4m3")[:, unstriped(offs)]
    w4 = unpack_weight(w4_words, w4_scales, "e2m1")
    a = mxq(f64(w1), 0, "e4m3").T @ v
    b = w4.T @ v
    d = a - b - f64(c)[:, None]
    h = f64(gain)[:, None] * np.square(d)
    y = mxq(f64(wm), 0, "e4m3").T @ mxq(h, 0, "e4m3")
    return np.sqrt(y)

@@ -1,0 +1,244 @@
+from contextlib import ExitStack
+
+import concourse.mybir as mybir
+from concourse.masks import make_identity
+
+K, H, N, T, S = 2048, 512, 512, 4096, 1024
+FLOPS = 2 * (2 * K * H * S + H * N * S)
+
+F32 = mybir.dt.float32
+BF16 = mybir.dt.bfloat16
+I32 = mybir.dt.int32
+U32 = mybir.dt.uint32
+U16 = mybir.dt.uint16
+U8 = mybir.dt.uint8
+FP8X4 = mybir.dt.float8_e4m3fn_x4
+FP4X4 = mybir.dt.float4_e2m1fn_x4
+ACT = mybir.ActivationFunctionType
+ALU = mybir.AluOpType
+AXIS = mybir.AxisListType
+
+P = 128
+PACK = 4
+PASSES = K // (P * PACK)
+HALF = 512
+HALVES = S // HALF
+SHIFT_ROWS = 112
+
+
+def tile_list_contrast_metric_distance_kernel(
+    tc, tab_words, tab_scales, offs, w1, w4_words, w4_scales, c, gain, wm, out
+):
+    nc = tc.nc
+    with ExitStack() as ctx:
+        keep = ctx.enter_context(tc.tile_pool(name="keep", bufs=1))
+        psum = ctx.enter_context(tc.psum_pool(name="psum", bufs=1))
+
+        def tile(shape, dtype, name):
+            return keep.tile(shape, dtype, name=name, align_bytes=64)
+
+        offsets = keep.tile([P, S // 16], U16, name="offsets")
+        nc.sync.dma_start(offsets[:], offs)
+
+        warm = tile([P, 1], F32, "warm")
+        warm_out = tile([P, 1], F32, "warm_out")
+        nc.vector.memset(warm[:], 1.0)
+        nc.scalar.activation(warm_out[:], warm[:], ACT.Sqrt)
+
+        tab_scale_rows = tile([P, T // 4], I32, "tab_scale_rows")
+        w4_scale_rows = tile([P, PASSES * H // 4], I32, "w4_scale_rows")
+        nc.vector.memset(tab_scale_rows[:], 0)
+        nc.vector.memset(w4_scale_rows[:], 0)
+        shifted = [None] + [tile([P, S // 4], I32, "shifted%d" % a) for a in range(1, PASSES)]
+        for a in range(1, PASSES):
+            nc.vector.memset(shifted[a][96:P, :], 0)
+        for q in range(4):
+            nc.gpsimd.dma_start(
+                tab_scale_rows[32 * q : 32 * q + 16, :], tab_scales[:, 4 * q : 4 * q + 4, :].bitcast(I32)
+            )
+        for q in range(4):
+            nc.gpsimd.dma_start(
+                w4_scale_rows[32 * q : 32 * q + 4, :].rearrange("r (a e) -> r a e", a=PASSES),
+                w4_scales[:, 4 * q : 4 * q + 4, :].rearrange("a r e -> r a e").bitcast(I32),
+            )
+
+        tab = [tile([P, T], I32, "tab%d" % a) for a in range(PASSES)]
+        w1_raw = [tile([P, PACK, H], F32, "w1_raw%d" % a) for a in range(PASSES)]
+        w4_raw = tile([P, PASSES * H // 2], I32, "w4_raw")
+        wm_raw = tile([P, PACK, N], F32, "wm_raw")
+        for a in range(PASSES):
+            nc.sync.dma_start(tab[a][:], tab_words[a].rearrange("p t i -> p (t i)").bitcast(I32))
+            if a == 0:
+                nc.sync.dma_start(
+                    w4_raw[:].rearrange("p (a e) -> p a e", a=PASSES),
+                    w4_words.rearrange("a p e -> p a e").bitcast(I32),
+                )
+            nc.sync.dma_start(w1_raw[a][:], w1[512 * a : 512 * (a + 1), :].rearrange("(p i) r -> p i r", i=PACK))
+        wm_rows = wm.rearrange("(q t b) n -> b q t n", t=4, b=4)
+        for b in range(4):
+            nc.sync.dma_start(wm_raw[b:P:4, :, :], wm_rows[b])
+
+        picked_scales = tile([P, S], U8, "picked_scales")
+        nc.vector.tensor_copy(picked_scales[:], tab_scale_rows[:].bitcast(U8).indirect(offsets[:]))
+        for a in range(1, PASSES):
+            nc.gpsimd.dma_start(shifted[a][0:SHIFT_ROWS, :], picked_scales[4 * a : 4 * a + SHIFT_ROWS, :].bitcast(I32))
+
+        wide = tile([P, 2, 16], F32, "wide")
+        for v, vec in enumerate((gain, c)):
+            nc.gpsimd.dma_start(
+                wide[:, v, :], vec.rearrange("(q x) -> q x", x=16).unsqueeze(1).to_broadcast([32, 4, 16])
+            )
+        ident = tile([P, P], F32, "ident")
+        make_identity(nc, ident[:])
+        own = tile([P, 4], F32, "own")
+        nc.vector.tensor_reduce(own[:], ident[:].rearrange("p (q b) -> p b q", b=4), AXIS.X, ALU.add)
+        masked = tile([P, 8, 4], F32, "masked")
+        nc.vector.tensor_tensor(
+            masked[:],
+            wide[:].rearrange("p v (t b) -> p (v t) b", b=4),
+            own[:].unsqueeze(1).to_broadcast([P, 8, 4]),
+            ALU.mult,
+        )
+        chan = tile([P, 8], F32, "chan")
+        nc.vector.tensor_reduce(chan[:], masked[:], AXIS.X, ALU.add)
+        gain_sb, c_sb = chan[:, 0:4], chan[:, 4:8]
+
+        w4_codes = tile([P, PASSES * H // 2], I32, "w4_codes")
+        w4_plane = tile([P, PASSES * H // 4], I32, "w4_plane")
+        nc.vector.tensor_copy(
+            w4_codes[:].rearrange("p (t m w) -> p t m w", t=4, w=2),
+            w4_raw[:].rearrange("p (m t w) -> p t m w", t=4, w=2),
+        )
+        nc.vector.tensor_copy(
+            w4_plane[:].rearrange("p (t m) -> p t m", t=4),
+            w4_scale_rows[:].rearrange("p (m t) -> p t m", t=4),
+        )
+
+        banks = [[psum.tile([P, HALF], F32, name="bank%d%d" % (h, t)) for t in range(4)] for h in range(HALVES)]
+        picked = [[tile([P, HALF], U32, "picked%d%d" % (a, h)) for h in range(HALVES)] for a in range(PASSES)]
+        w1_bf = [tile([P, PACK * H], BF16, "w1_bf%d" % a) for a in range(PASSES)]
+        w1_codes = [tile([P, H], U32, "w1_codes%d" % a) for a in range(PASSES)]
+        w1_plane = [tile([P, H], U8, "w1_plane%d" % a) for a in range(PASSES)]
+
+        def gather(a, h):
+            cols = offsets[:, h * (HALF // 16) : (h + 1) * (HALF // 16)]
+            nc.vector.tensor_copy(picked[a][h][:], tab[a][:].bitcast(U32).indirect(cols))
+
+        def w1_views(a, t):
+            dst = w1_bf[a][:, 512 * t : 512 * (t + 1)].rearrange("p (q b i) -> p q i b", b=4, i=PACK)
+            src = w1_raw[a][:].rearrange("p i (q t b) -> p t q i b", t=4, b=4)[:, t]
+            return dst, src
+
+        def w1_quantize(a, t0, t1):
+            nc.vector.quantize_mx(
+                out=w1_codes[a][:, P * t0 : P * t1].bitcast(FP8X4),
+                scales=w1_plane[a][:, P * t0 : P * t1],
+                in_=w1_bf[a][:, 512 * t0 : 512 * t1],
+            )
+
+        def pass_w4(a, h, t):
+            cols = slice(h * HALF, (h + 1) * HALF)
+            plane = picked_scales[:, cols] if a == 0 else shifted[a][:].bitcast(U8)[:, cols]
+            col0 = (t * PASSES + a) * P
+            nc.tensor.matmul_mx(
+                out=banks[h][t][:],
+                lhsT=w4_codes[:, col0 // 2 : (col0 + P) // 2].bitcast(FP4X4),
+                lhsT_scale=w4_plane[:, col0 // 4 : (col0 + P) // 4].bitcast(U8),
+                rhs=picked[a][h][:].bitcast(FP8X4),
+                rhs_scale=plane,
+                start=(a == 0),
+                stop=False,
+            )
+
+        def pass_w1(a, h, t):
+            nc.tensor.matmul_mx(
+                out=banks[h][t][:],
+                lhsT=w1_codes[a][:, P * t : P * (t + 1)].bitcast(FP8X4),
+                lhsT_scale=w1_plane[a][:, P * t : P * (t + 1)],
+                rhs=picked[a][h][:].bitcast(FP8X4),
+                rhs_scale=picked_scales[4 * a : P, h * HALF : (h + 1) * HALF],
+                start=False,
+                stop=(a == PASSES - 1),
+            )
+
+        last = PASSES - 1
+        for a in range(last):
+            for h in range(HALVES):
+                gather(a, h)
+            for t in range(4):
+                dst, src = w1_views(a, t)
+                nc.scalar.activation(dst, src, ACT.Copy, scale=-1.0)
+            w1_quantize(a, 0, 4)
+            for h in range(HALVES):
+                for t in range(4):
+                    pass_w4(a, h, t)
+            for h in range(HALVES):
+                for t in range(4):
+                    pass_w1(a, h, t)
+
+        root0 = tile([P, 4], F32, "root0")
+        inv = tile([P, 4], F32, "inv")
+        quot = tile([P, 4], F32, "quot")
+        both = tile([P, 4], F32, "both")
+        root = tile([P, 4], F32, "root")
+        bias = tile([P, 4], F32, "bias")
+        nc.scalar.activation(root0[:], gain_sb, ACT.Sqrt)
+        nc.vector.reciprocal(inv[:], root0[:])
+        nc.vector.tensor_tensor(quot[:], gain_sb, inv[:], ALU.mult)
+        nc.vector.tensor_tensor(both[:], quot[:], root0[:], ALU.add)
+        nc.vector.tensor_scalar(root[:], both[:], 0.5, None, ALU.mult)
+        nc.vector.tensor_tensor(bias[:], root[:], c_sb, ALU.mult)
+
+        for h in range(HALVES):
+            gather(last, h)
+        for t in range(5):
+            if t < 4:
+                dst, src = w1_views(last, t)
+                nc.vector.tensor_scalar(dst, src, -1.0, None, ALU.mult)
+            if t > 0:
+                w1_quantize(last, t - 1, t)
+        for h in range(HALVES):
+            for t in range(4):
+                pass_w4(last, h, t)
+            for t in range(4):
+                pass_w1(last, h, t)
+
+        wm_bf = tile([P, PACK * N], BF16, "wm_bf")
+        wm_codes = tile([P, N], U32, "wm_codes")
+        wm_plane = tile([P, N], U8, "wm_plane")
+        nc.vector.tensor_copy(
+            wm_bf[:].rearrange("p (m j t) -> p m t j", j=4, t=PACK),
+            wm_raw[:].rearrange("p t (m j) -> p m t j", j=4),
+        )
+        nc.vector.quantize_mx(out=wm_codes[:].bitcast(FP8X4), scales=wm_plane[:], in_=wm_bf[:])
+
+        h_codes = [tile([P, HALF], U32, "h_codes%d" % h) for h in range(HALVES)]
+        h_plane = [tile([P, HALF], U8, "h_plane%d" % h) for h in range(HALVES)]
+        for h in range(HALVES):
+            h_rows = tile([P, PACK, HALF], BF16, "h_rows%d" % h)
+            h_bf = tile([P, PACK * HALF], BF16, "h_bf%d" % h)
+            for t in range(4):
+                nc.scalar.activation(
+                    h_rows[:, t, :], banks[h][t][:], ACT.Square, bias=bias[:, t : t + 1], scale=root[:, t : t + 1]
+                )
+            nc.vector.tensor_copy(
+                h_bf[:].rearrange("p (m j t) -> p m t j", j=4, t=PACK),
+                h_rows[:].rearrange("p t (m j) -> p m t j", j=4),
+            )
+            nc.vector.quantize_mx(out=h_codes[h][:].bitcast(FP8X4), scales=h_plane[h][:], in_=h_bf[:])
+
+        for h in range(HALVES):
+            for u in range(N // P):
+                acc = psum.tile([P, HALF], F32, name="bank%d%d" % (h, u))
+                nc.tensor.matmul_mx(
+                    out=acc[:],
+                    lhsT=wm_codes[:, P * u : P * (u + 1)].bitcast(FP8X4),
+                    lhsT_scale=wm_plane[:, P * u : P * (u + 1)],
+                    rhs=h_codes[h][:].bitcast(FP8X4),
+                    rhs_scale=h_plane[h][:],
+                    start=True,
+                    stop=True,
+                )
+                dist = tile([P, HALF], F32, "dist%d%d" % (h, u))
+                nc.scalar.activation(dist[:], acc[:], ACT.Sqrt)
+                nc.sync.dma_start(out[P * u : P * (u + 1), h * HALF : (h + 1) * HALF], dist[:])

@@ -34,8 +34,8 @@ def tile_list_contrast_metric_distance_kernel(
         keep = ctx.enter_context(tc.tile_pool(name="keep", bufs=1))
         psum = ctx.enter_context(tc.psum_pool(name="psum", bufs=1))
 
-        def tile(shape, dtype, name):
-            return keep.tile(shape, dtype, name=name, align_bytes=64)
+        def tile(shape, dtype, name, tag=None):
+            return keep.tile(shape, dtype, name=name, tag=tag or name, align_bytes=64)
 
         offsets = keep.tile([P, S // 16], U16, name="offsets")
         nc.sync.dma_start(offsets[:], offs)
@@ -115,14 +115,14 @@ def tile_list_contrast_metric_distance_kernel(
         )
 
         banks = [[psum.tile([P, HALF], F32, name="bank%d%d" % (h, t)) for t in range(4)] for h in range(HALVES)]
-        picked = [[tile([P, HALF], U32, "picked%d%d" % (a, h)) for h in range(HALVES)] for a in range(PASSES)]
-        w1_bf = [tile([P, PACK * H], BF16, "w1_bf%d" % a) for a in range(PASSES)]
+        picked = []
+        w1_bf = []
         w1_codes = [tile([P, H], U32, "w1_codes%d" % a) for a in range(PASSES)]
         w1_plane = [tile([P, H], U8, "w1_plane%d" % a) for a in range(PASSES)]
 
         def gather(a, h):
             cols = offsets[:, h * (HALF // 16) : (h + 1) * (HALF // 16)]
-            nc.vector.tensor_copy(picked[a][h][:], tab[a][:].bitcast(U32).indirect(cols))
+            nc.vector.tensor_copy(picked[a][:, h * HALF : (h + 1) * HALF], tab[a][:].bitcast(U32).indirect(cols))
 
         def w1_views(a, t):
             dst = w1_bf[a][:, 512 * t : 512 * (t + 1)].rearrange("p (q b i) -> p q i b", b=4, i=PACK)
@@ -144,7 +144,7 @@ def tile_list_contrast_metric_distance_kernel(
                 out=banks[h][t][:],
                 lhsT=w4_codes[:, col0 // 2 : (col0 + P) // 2].bitcast(FP4X4),
                 lhsT_scale=w4_plane[:, col0 // 4 : (col0 + P) // 4].bitcast(U8),
-                rhs=picked[a][h][:].bitcast(FP8X4),
+                rhs=picked[a][:, h * HALF : (h + 1) * HALF].bitcast(FP8X4),
                 rhs_scale=plane,
                 start=(a == 0),
                 stop=False,
@@ -155,7 +155,7 @@ def tile_list_contrast_metric_distance_kernel(
                 out=banks[h][t][:],
                 lhsT=w1_codes[a][:, P * t : P * (t + 1)].bitcast(FP8X4),
                 lhsT_scale=w1_plane[a][:, P * t : P * (t + 1)],
-                rhs=picked[a][h][:].bitcast(FP8X4),
+                rhs=picked[a][:, h * HALF : (h + 1) * HALF].bitcast(FP8X4),
                 rhs_scale=picked_scales[4 * a : P, h * HALF : (h + 1) * HALF],
                 start=False,
                 stop=(a == PASSES - 1),
@@ -163,8 +163,10 @@ def tile_list_contrast_metric_distance_kernel(
 
         last = PASSES - 1
         for a in range(last):
+            picked.append(tile([P, S], U32, "picked%d" % a, "turn%d" % a))
             for h in range(HALVES):
                 gather(a, h)
+            w1_bf.append(tile([P, PACK * H], BF16, "w1_bf%d" % a, "turn%d" % (a + 1)))
             for t in range(4):
                 dst, src = w1_views(a, t)
                 nc.scalar.activation(dst, src, ACT.Copy, scale=-1.0)
@@ -189,8 +191,10 @@ def tile_list_contrast_metric_distance_kernel(
         nc.vector.tensor_scalar(root[:], both[:], 0.5, None, ALU.mult)
         nc.vector.tensor_tensor(bias[:], root[:], c_sb, ALU.mult)
 
+        picked.append(tile([P, S], U32, "picked%d" % last, "turn%d" % last))
         for h in range(HALVES):
             gather(last, h)
+        w1_bf.append(tile([P, PACK * H], BF16, "w1_bf%d" % last, "tab%d" % last))
         for t in range(5):
             if t < 4:
                 dst, src = w1_views(last, t)
@@ -203,7 +207,7 @@ def tile_list_contrast_metric_distance_kernel(
             for t in range(4):
                 pass_w1(last, h, t)
 
-        wm_bf = tile([P, PACK * N], BF16, "wm_bf")
+        wm_bf = tile([P, PACK * N], BF16, "wm_bf", "tab%d" % last)
         wm_codes = tile([P, N], U32, "wm_codes")
         wm_plane = tile([P, N], U8, "wm_plane")
         nc.vector.tensor_copy(

@@ -23,6 +23,8 @@ PACK = 4
 PASSES = K // (P * PACK)
 HALF = 512
 HALVES = S // HALF
+PART = 256
+PARTS = S // PART
 SHIFT_ROWS = 112
 
 
@@ -37,62 +39,43 @@ def tile_list_contrast_metric_distance_kernel(
         def tile(shape, dtype, name, tag=None):
             return keep.tile(shape, dtype, name=name, tag=tag or name, align_bytes=64)
 
+        tab = {}
+        w1_raw = {}
+
+        def load_tab(a, tag):
+            tab[a] = tile([P, T], I32, "tab%d" % a, tag)
+            nc.sync.dma_start(tab[a][:], tab_words[a].rearrange("p t i -> p (t i)").bitcast(I32))
+
+        def load_w1(a, tag):
+            w1_raw[a] = tile([P, PACK, H], F32, "w1_raw%d" % a, tag)
+            nc.sync.dma_start(w1_raw[a][:], w1[512 * a : 512 * (a + 1), :].rearrange("(p i) r -> p i r", i=PACK))
+
+        wide = tile([P, 2, 16], F32, "wide", "slot_d")
+        for v, vec in enumerate((gain, c)):
+            nc.sync.dma_start(
+                wide[:, v, :], vec.rearrange("(q x) -> q x", x=16).unsqueeze(1).to_broadcast([32, 4, 16])
+            )
+
+        load_tab(0, "slot_a")
         offsets = keep.tile([P, S // 16], U16, name="offsets")
         nc.sync.dma_start(offsets[:], offs)
 
-        warm = tile([P, 1], F32, "warm")
-        warm_out = tile([P, 1], F32, "warm_out")
-        nc.vector.memset(warm[:], 1.0)
-        nc.scalar.activation(warm_out[:], warm[:], ACT.Sqrt)
-
-        tab_scale_rows = tile([P, T // 4], I32, "tab_scale_rows")
-        w4_scale_rows = tile([P, PASSES * H // 4], I32, "w4_scale_rows")
+        tab_scale_rows = tile([P, T // 4], I32, "tab_scale_rows", "slot_b")
         nc.vector.memset(tab_scale_rows[:], 0)
-        nc.vector.memset(w4_scale_rows[:], 0)
         shifted = [None] + [tile([P, S // 4], I32, "shifted%d" % a) for a in range(1, PASSES)]
-        for a in range(1, PASSES):
-            nc.vector.memset(shifted[a][96:P, :], 0)
         for q in range(4):
-            nc.gpsimd.dma_start(
+            nc.sync.dma_start(
                 tab_scale_rows[32 * q : 32 * q + 16, :], tab_scales[:, 4 * q : 4 * q + 4, :].bitcast(I32)
             )
-        for q in range(4):
-            nc.gpsimd.dma_start(
-                w4_scale_rows[32 * q : 32 * q + 4, :].rearrange("r (a e) -> r a e", a=PASSES),
-                w4_scales[:, 4 * q : 4 * q + 4, :].rearrange("a r e -> r a e").bitcast(I32),
-            )
-
-        tab = [tile([P, T], I32, "tab%d" % a) for a in range(PASSES)]
-        w1_raw = [tile([P, PACK, H], F32, "w1_raw%d" % a) for a in range(PASSES)]
-        w4_raw = tile([P, PASSES * H // 2], I32, "w4_raw")
-        wm_raw = tile([P, PACK, N], F32, "wm_raw")
-        for a in range(PASSES):
-            nc.sync.dma_start(tab[a][:], tab_words[a].rearrange("p t i -> p (t i)").bitcast(I32))
-            if a == 0:
-                nc.sync.dma_start(
-                    w4_raw[:].rearrange("p (a e) -> p a e", a=PASSES),
-                    w4_words.rearrange("a p e -> p a e").bitcast(I32),
-                )
-            nc.sync.dma_start(w1_raw[a][:], w1[512 * a : 512 * (a + 1), :].rearrange("(p i) r -> p i r", i=PACK))
-        wm_rows = wm.rearrange("(q t b) n -> b q t n", t=4, b=4)
-        for b in range(4):
-            nc.sync.dma_start(wm_raw[b:P:4, :, :], wm_rows[b])
-
-        picked_scales = tile([P, S], U8, "picked_scales")
-        nc.vector.tensor_copy(picked_scales[:], tab_scale_rows[:].bitcast(U8).indirect(offsets[:]))
-        for a in range(1, PASSES):
-            nc.gpsimd.dma_start(shifted[a][0:SHIFT_ROWS, :], picked_scales[4 * a : 4 * a + SHIFT_ROWS, :].bitcast(I32))
-
-        wide = tile([P, 2, 16], F32, "wide")
-        for v, vec in enumerate((gain, c)):
-            nc.gpsimd.dma_start(
-                wide[:, v, :], vec.rearrange("(q x) -> q x", x=16).unsqueeze(1).to_broadcast([32, 4, 16])
-            )
-        ident = tile([P, P], F32, "ident")
+        ident = tile([P, P], F32, "ident", "slot_c")
         make_identity(nc, ident[:])
         own = tile([P, 4], F32, "own")
         nc.vector.tensor_reduce(own[:], ident[:].rearrange("p (q b) -> p b q", b=4), AXIS.X, ALU.add)
-        masked = tile([P, 8, 4], F32, "masked")
+
+        load_w1(0, "slot_c")
+        for a in range(1, PASSES):
+            nc.vector.memset(shifted[a][96:P, :], 0)
+        masked = tile([P, 8, 4], F32, "masked", "slot_e")
         nc.vector.tensor_tensor(
             masked[:],
             wide[:].rearrange("p v (t b) -> p (v t) b", b=4),
@@ -103,16 +86,31 @@ def tile_list_contrast_metric_distance_kernel(
         nc.vector.tensor_reduce(chan[:], masked[:], AXIS.X, ALU.add)
         gain_sb, c_sb = chan[:, 0:4], chan[:, 4:8]
 
-        w4_codes = tile([P, PASSES * H // 2], I32, "w4_codes")
-        w4_plane = tile([P, PASSES * H // 4], I32, "w4_plane")
-        nc.vector.tensor_copy(
-            w4_codes[:].rearrange("p (t m w) -> p t m w", t=4, w=2),
-            w4_raw[:].rearrange("p (m t w) -> p t m w", t=4, w=2),
+        w4_raw = tile([P, PASSES * H // 2], I32, "w4_raw", "slot_d")
+        nc.sync.dma_start(
+            w4_raw[:].rearrange("p (a e) -> p a e", a=PASSES), w4_words.rearrange("a p e -> p a e").bitcast(I32)
         )
-        nc.vector.tensor_copy(
-            w4_plane[:].rearrange("p (t m) -> p t m", t=4),
-            w4_scale_rows[:].rearrange("p (m t) -> p t m", t=4),
-        )
+
+        w4_scale_rows = tile([P, PASSES * H // 4], I32, "w4_scale_rows", "slot_e")
+        nc.vector.memset(w4_scale_rows[:], 0)
+        for q in range(4):
+            nc.sync.dma_start(
+                w4_scale_rows[32 * q : 32 * q + 4, :].rearrange("r (a e) -> r a e", a=PASSES),
+                w4_scales[:, 4 * q : 4 * q + 4, :].rearrange("a r e -> r a e").bitcast(I32),
+            )
+
+        root0 = tile([P, 4], F32, "root0")
+        inv = tile([P, 4], F32, "inv")
+        quot = tile([P, 4], F32, "quot")
+        both = tile([P, 4], F32, "both")
+        root = tile([P, 4], F32, "root")
+        bias = tile([P, 4], F32, "bias")
+        nc.scalar.activation(root0[:], gain_sb, ACT.Sqrt)
+        nc.vector.reciprocal(inv[:], root0[:])
+        nc.vector.tensor_tensor(quot[:], gain_sb, inv[:], ALU.mult)
+        nc.vector.tensor_tensor(both[:], quot[:], root0[:], ALU.add)
+        nc.vector.tensor_scalar(root[:], both[:], 0.5, None, ALU.mult)
+        nc.vector.tensor_tensor(bias[:], root[:], c_sb, ALU.mult)
 
         banks = [[psum.tile([P, HALF], F32, name="bank%d%d" % (h, t)) for t in range(4)] for h in range(HALVES)]
         picked = []
@@ -146,7 +144,7 @@ def tile_list_contrast_metric_distance_kernel(
                 lhsT_scale=w4_plane[:, col0 // 4 : (col0 + P) // 4].bitcast(U8),
                 rhs=picked[a][:, h * HALF : (h + 1) * HALF].bitcast(FP8X4),
                 rhs_scale=plane,
-                start=(a == 0),
+                start=False,
                 stop=False,
             )
 
@@ -157,92 +155,132 @@ def tile_list_contrast_metric_distance_kernel(
                 lhsT_scale=w1_plane[a][:, P * t : P * (t + 1)],
                 rhs=picked[a][:, h * HALF : (h + 1) * HALF].bitcast(FP8X4),
                 rhs_scale=picked_scales[4 * a : P, h * HALF : (h + 1) * HALF],
-                start=False,
+                start=(a == 0),
                 stop=(a == PASSES - 1),
             )
 
         last = PASSES - 1
+        picked.append(tile([P, S], U32, "picked0"))
+        for h in range(HALVES):
+            gather(0, h)
+        load_tab(1, "slot_a")
+        picked_scales = tile([P, S], U8, "picked_scales")
+        nc.vector.tensor_copy(picked_scales[:], tab_scale_rows[:].bitcast(U8).indirect(offsets[:]))
+        for a in range(1, PASSES):
+            nc.sync.dma_start(shifted[a][0:SHIFT_ROWS, :], picked_scales[4 * a : 4 * a + SHIFT_ROWS, :].bitcast(I32))
+
+        load_w1(1, "slot_b")
+        w4_codes = tile([P, PASSES * H // 2], I32, "w4_codes")
+        w4_plane = tile([P, PASSES * H // 4], I32, "w4_plane")
+        nc.vector.tensor_copy(
+            w4_codes[:].rearrange("p (t m w) -> p t m w", t=4, w=2),
+            w4_raw[:].rearrange("p (m t w) -> p t m w", t=4, w=2),
+        )
+        load_tab(2, "slot_d")
+        nc.vector.tensor_copy(
+            w4_plane[:].rearrange("p (t m) -> p t m", t=4),
+            w4_scale_rows[:].rearrange("p (m t) -> p t m", t=4),
+        )
+
         for a in range(last):
-            picked.append(tile([P, S], U32, "picked%d" % a, "turn%d" % a))
-            for h in range(HALVES):
-                gather(a, h)
+            if a > 0:
+                picked.append(tile([P, S], U32, "picked%d" % a, "turn%d" % a))
+                for h in range(HALVES):
+                    gather(a, h)
+                load_w1(a + 1, "slot_a" if a == 1 else "slot_d")
             w1_bf.append(tile([P, PACK * H], BF16, "w1_bf%d" % a, "turn%d" % (a + 1)))
             for t in range(4):
                 dst, src = w1_views(a, t)
-                nc.scalar.activation(dst, src, ACT.Copy, scale=-1.0)
-            w1_quantize(a, 0, 4)
-            for h in range(HALVES):
-                for t in range(4):
-                    pass_w4(a, h, t)
-            for h in range(HALVES):
-                for t in range(4):
-                    pass_w1(a, h, t)
+                if a > 0 and t % 2 == 0:
+                    nc.vector.tensor_scalar(dst, src, -1.0, None, ALU.mult)
+                else:
+                    nc.scalar.activation(dst, src, ACT.Copy, scale=-1.0)
+                if t % 2 == 1:
+                    w1_quantize(a, t - 1, t + 1)
+            if a == 1:
+                load_tab(last, "slot_b")
+            for one_pass in (pass_w1, pass_w4) if a == 0 else (pass_w4, pass_w1):
+                for h in range(HALVES):
+                    for t in range(4):
+                        one_pass(a, h, t)
 
-        root0 = tile([P, 4], F32, "root0")
-        inv = tile([P, 4], F32, "inv")
-        quot = tile([P, 4], F32, "quot")
-        both = tile([P, 4], F32, "both")
-        root = tile([P, 4], F32, "root")
-        bias = tile([P, 4], F32, "bias")
-        nc.scalar.activation(root0[:], gain_sb, ACT.Sqrt)
-        nc.vector.reciprocal(inv[:], root0[:])
-        nc.vector.tensor_tensor(quot[:], gain_sb, inv[:], ALU.mult)
-        nc.vector.tensor_tensor(both[:], quot[:], root0[:], ALU.add)
-        nc.vector.tensor_scalar(root[:], both[:], 0.5, None, ALU.mult)
-        nc.vector.tensor_tensor(bias[:], root[:], c_sb, ALU.mult)
+        wm_raw = tile([P, PACK, N], F32, "wm_raw", "slot_a")
+        wm_rows = wm.rearrange("(q t b) n -> b q t n", t=4, b=4)
+        for b in range(4):
+            nc.sync.dma_start(wm_raw[b:P:4, :, :], wm_rows[b])
 
         picked.append(tile([P, S], U32, "picked%d" % last, "turn%d" % last))
         for h in range(HALVES):
             gather(last, h)
-        w1_bf.append(tile([P, PACK * H], BF16, "w1_bf%d" % last, "tab%d" % last))
-        for t in range(5):
-            if t < 4:
-                dst, src = w1_views(last, t)
+        w1_bf.append(tile([P, PACK * H], BF16, "w1_bf%d" % last, "slot_b"))
+        for t in range(4):
+            dst, src = w1_views(last, t)
+            if t % 2 == 0:
                 nc.vector.tensor_scalar(dst, src, -1.0, None, ALU.mult)
-            if t > 0:
+            else:
+                nc.scalar.activation(dst, src, ACT.Copy, scale=-1.0)
                 w1_quantize(last, t - 1, t)
+                w1_quantize(last, t, t + 1)
         for h in range(HALVES):
             for t in range(4):
                 pass_w4(last, h, t)
             for t in range(4):
                 pass_w1(last, h, t)
 
-        wm_bf = tile([P, PACK * N], BF16, "wm_bf", "tab%d" % last)
+        wm_bf = tile([P, PACK * N], BF16, "wm_bf", "slot_b")
         wm_codes = tile([P, N], U32, "wm_codes")
         wm_plane = tile([P, N], U8, "wm_plane")
         nc.vector.tensor_copy(
             wm_bf[:].rearrange("p (m j t) -> p m t j", j=4, t=PACK),
             wm_raw[:].rearrange("p t (m j) -> p m t j", j=4),
         )
-        nc.vector.quantize_mx(out=wm_codes[:].bitcast(FP8X4), scales=wm_plane[:], in_=wm_bf[:])
 
-        h_codes = [tile([P, HALF], U32, "h_codes%d" % h) for h in range(HALVES)]
-        h_plane = [tile([P, HALF], U8, "h_plane%d" % h) for h in range(HALVES)]
+        h_rows = [tile([P, PACK, HALF], BF16, "h_rows%d" % h) for h in range(HALVES)]
         for h in range(HALVES):
-            h_rows = tile([P, PACK, HALF], BF16, "h_rows%d" % h)
-            h_bf = tile([P, PACK * HALF], BF16, "h_bf%d" % h)
             for t in range(4):
                 nc.scalar.activation(
-                    h_rows[:, t, :], banks[h][t][:], ACT.Square, bias=bias[:, t : t + 1], scale=root[:, t : t + 1]
+                    h_rows[h][:, t, :], banks[h][t][:], ACT.Square, bias=bias[:, t : t + 1], scale=root[:, t : t + 1]
                 )
-            nc.vector.tensor_copy(
-                h_bf[:].rearrange("p (m j t) -> p m t j", j=4, t=PACK),
-                h_rows[:].rearrange("p t (m j) -> p m t j", j=4),
-            )
-            nc.vector.quantize_mx(out=h_codes[h][:].bitcast(FP8X4), scales=h_plane[h][:], in_=h_bf[:])
 
-        for h in range(HALVES):
-            for u in range(N // P):
-                acc = psum.tile([P, HALF], F32, name="bank%d%d" % (h, u))
-                nc.tensor.matmul_mx(
-                    out=acc[:],
-                    lhsT=wm_codes[:, P * u : P * (u + 1)].bitcast(FP8X4),
-                    lhsT_scale=wm_plane[:, P * u : P * (u + 1)],
-                    rhs=h_codes[h][:].bitcast(FP8X4),
-                    rhs_scale=h_plane[h][:],
-                    start=True,
-                    stop=True,
-                )
-                dist = tile([P, HALF], F32, "dist%d%d" % (h, u))
+        h_bf = {}
+        h_codes = [tile([P, PART], U32, "h_codes%d" % j) for j in range(PARTS)]
+        h_plane = [tile([P, PART], U8, "h_plane%d" % j) for j in range(PARTS)]
+
+        def h_interleave(j):
+            h_bf[j] = tile([P, PACK * PART], BF16, "h_bf%d" % j, "slot_a" if j % 2 == 0 else "slot_b")
+            cols = slice((j % 2) * PART, (j % 2 + 1) * PART)
+            nc.vector.tensor_copy(
+                h_bf[j][:].rearrange("p (m i t) -> p m t i", i=4, t=PACK),
+                h_rows[j // 2][:, :, cols].rearrange("p t (m i) -> p m t i", i=4),
+            )
+
+        def h_quantize(j):
+            nc.vector.quantize_mx(out=h_codes[j][:].bitcast(FP8X4), scales=h_plane[j][:], in_=h_bf[j][:])
+
+        h_interleave(0)
+        nc.vector.quantize_mx(out=wm_codes[:].bitcast(FP8X4), scales=wm_plane[:], in_=wm_bf[:])
+        h_quantize(0)
+        h_interleave(1)
+        for j in range(1, PARTS):
+            if j + 1 < PARTS:
+                h_interleave(j + 1)
+            h_quantize(j)
+
+        out_rows = out.rearrange("(u p) j -> p u j", p=P)
+        for j in range(PARTS):
+            for pair in range(2):
+                acc = psum.tile([P, 2, PART], F32, name="bank%d%d" % (j // 2, 2 * (j % 2) + pair))
+                for e in range(2):
+                    u = 2 * pair + e
+                    nc.tensor.matmul_mx(
+                        out=acc[:, e, :],
+                        lhsT=wm_codes[:, P * u : P * (u + 1)].bitcast(FP8X4),
+                        lhsT_scale=wm_plane[:, P * u : P * (u + 1)],
+                        rhs=h_codes[j][:].bitcast(FP8X4),
+                        rhs_scale=h_plane[j][:],
+                        start=True,
+                        stop=True,
+                    )
+                dist = tile([P, 2, PART], F32, "dist%d%d" % (j, pair))
                 nc.scalar.activation(dist[:], acc[:], ACT.Sqrt)
-                nc.sync.dma_start(out[P * u : P * (u + 1), h * HALF : (h + 1) * HALF], dist[:])
+                nc.sync.dma_start(out_rows[:, 2 * pair : 2 * pair + 2, j * PART : (j + 1) * PART], dist[:])

@@ -1,7 +1,6 @@
 from contextlib import ExitStack
 
 import concourse.mybir as mybir
-from concourse.masks import make_identity
 
 K, H, N, T, S = 2048, 512, 512, 4096, 1024
 FLOPS = 2 * (2 * K * H * S + H * N * S)
@@ -16,7 +15,6 @@ FP8X4 = mybir.dt.float8_e4m3fn_x4
 FP4X4 = mybir.dt.float4_e2m1fn_x4
 ACT = mybir.ActivationFunctionType
 ALU = mybir.AluOpType
-AXIS = mybir.AxisListType
 
 P = 128
 PACK = 4
@@ -50,12 +48,10 @@ def tile_list_contrast_metric_distance_kernel(
             w1_raw[a] = tile([P, PACK, H], F32, "w1_raw%d" % a, tag)
             nc.sync.dma_start(w1_raw[a][:], w1[512 * a : 512 * (a + 1), :].rearrange("(p i) r -> p i r", i=PACK))
 
-        wide = tile([P, 2, 16], F32, "wide", "slot_d")
-        for v, vec in enumerate((gain, c)):
-            nc.sync.dma_start(
-                wide[:, v, :], vec.rearrange("(q x) -> q x", x=16).unsqueeze(1).to_broadcast([32, 4, 16])
-            )
-
+        gain_sb = tile([P, 4], F32, "gain_sb")
+        c_sb = tile([P, 4], F32, "c_sb")
+        nc.sync.dma_start(gain_sb[:], gain.rearrange("(p t) -> p t", t=4))
+        nc.sync.dma_start(c_sb[:], c.rearrange("(p t) -> p t", t=4))
         load_tab(0, "slot_a")
         offsets = keep.tile([P, S // 16], U16, name="offsets")
         nc.sync.dma_start(offsets[:], offs)
@@ -67,25 +63,22 @@ def tile_list_contrast_metric_distance_kernel(
             nc.sync.dma_start(
                 tab_scale_rows[32 * q : 32 * q + 16, :], tab_scales[:, 4 * q : 4 * q + 4, :].bitcast(I32)
             )
-        ident = tile([P, P], F32, "ident", "slot_c")
-        make_identity(nc, ident[:])
-        own = tile([P, 4], F32, "own")
-        nc.vector.tensor_reduce(own[:], ident[:].rearrange("p (q b) -> p b q", b=4), AXIS.X, ALU.add)
-
-        load_w1(0, "slot_c")
         for a in range(1, PASSES):
             nc.vector.memset(shifted[a][96:P, :], 0)
-        masked = tile([P, 8, 4], F32, "masked", "slot_e")
-        nc.vector.tensor_tensor(
-            masked[:],
-            wide[:].rearrange("p v (t b) -> p (v t) b", b=4),
-            own[:].unsqueeze(1).to_broadcast([P, 8, 4]),
-            ALU.mult,
-        )
-        chan = tile([P, 8], F32, "chan")
-        nc.vector.tensor_reduce(chan[:], masked[:], AXIS.X, ALU.add)
-        gain_sb, c_sb = chan[:, 0:4], chan[:, 4:8]
+        root0 = tile([P, 4], F32, "root0")
+        inv = tile([P, 4], F32, "inv", "slot_c")
+        quot = tile([P, 4], F32, "quot", "slot_d")
+        both = tile([P, 4], F32, "both", "slot_e")
+        root = tile([P, 4], F32, "root")
+        bias = tile([P, 4], F32, "bias")
+        nc.scalar.activation(root0[:], gain_sb[:], ACT.Sqrt)
+        nc.vector.reciprocal(inv[:], root0[:])
+        nc.vector.tensor_tensor(quot[:], gain_sb[:], inv[:], ALU.mult)
+        nc.vector.tensor_tensor(both[:], quot[:], root0[:], ALU.add)
+        nc.vector.tensor_scalar(root[:], both[:], 0.5, None, ALU.mult)
+        nc.vector.tensor_tensor(bias[:], root[:], c_sb[:], ALU.mult)
 
+        load_w1(0, "slot_c")
         w4_raw = tile([P, PASSES * H // 2], I32, "w4_raw", "slot_d")
         nc.sync.dma_start(
             w4_raw[:].rearrange("p (a e) -> p a e", a=PASSES), w4_words.rearrange("a p e -> p a e").bitcast(I32)
@@ -93,24 +86,11 @@ def tile_list_contrast_metric_distance_kernel(
 
         w4_scale_rows = tile([P, PASSES * H // 4], I32, "w4_scale_rows", "slot_e")
         nc.vector.memset(w4_scale_rows[:], 0)
-        for q in range(4):
+        w4_scales_by_row = w4_scales.rearrange("a (q r) e -> r q a e", r=4)
+        for r in range(4):
             nc.sync.dma_start(
-                w4_scale_rows[32 * q : 32 * q + 4, :].rearrange("r (a e) -> r a e", a=PASSES),
-                w4_scales[:, 4 * q : 4 * q + 4, :].rearrange("a r e -> r a e").bitcast(I32),
+                w4_scale_rows[r:P:32, :].rearrange("q (a e) -> q a e", a=PASSES), w4_scales_by_row[r].bitcast(I32)
             )
-
-        root0 = tile([P, 4], F32, "root0")
-        inv = tile([P, 4], F32, "inv")
-        quot = tile([P, 4], F32, "quot")
-        both = tile([P, 4], F32, "both")
-        root = tile([P, 4], F32, "root")
-        bias = tile([P, 4], F32, "bias")
-        nc.scalar.activation(root0[:], gain_sb, ACT.Sqrt)
-        nc.vector.reciprocal(inv[:], root0[:])
-        nc.vector.tensor_tensor(quot[:], gain_sb, inv[:], ALU.mult)
-        nc.vector.tensor_tensor(both[:], quot[:], root0[:], ALU.add)
-        nc.vector.tensor_scalar(root[:], both[:], 0.5, None, ALU.mult)
-        nc.vector.tensor_tensor(bias[:], root[:], c_sb, ALU.mult)
 
         banks = [[psum.tile([P, HALF], F32, name="bank%d%d" % (h, t)) for t in range(4)] for h in range(HALVES)]
         picked = []
@@ -122,17 +102,20 @@ def tile_list_contrast_metric_distance_kernel(
             cols = offsets[:, h * (HALF // 16) : (h + 1) * (HALF // 16)]
             nc.vector.tensor_copy(picked[a][:, h * HALF : (h + 1) * HALF], tab[a][:].bitcast(U32).indirect(cols))
 
-        def w1_views(a, t):
-            dst = w1_bf[a][:, 512 * t : 512 * (t + 1)].rearrange("p (q b i) -> p q i b", b=4, i=PACK)
-            src = w1_raw[a][:].rearrange("p i (q t b) -> p t q i b", t=4, b=4)[:, t]
-            return dst, src
-
-        def w1_quantize(a, t0, t1):
-            nc.vector.quantize_mx(
-                out=w1_codes[a][:, P * t0 : P * t1].bitcast(FP8X4),
-                scales=w1_plane[a][:, P * t0 : P * t1],
-                in_=w1_bf[a][:, 512 * t0 : 512 * t1],
-            )
+        def w1_prepare(a):
+            for g in range(2):
+                dst = w1_bf[a][:, 1024 * g : 1024 * (g + 1)].rearrange("p (t m i) -> p m t i", t=2, i=PACK)
+                src = w1_raw[a][:].rearrange("p i (m t) -> p m t i", t=4)[:, :, 2 * g : 2 * g + 2, :]
+                if a > 0 and g == 0:
+                    nc.vector.tensor_scalar(dst, src, -1.0, None, ALU.mult)
+                else:
+                    nc.scalar.activation(dst, src, ACT.Copy, scale=-1.0)
+            for g in range(2):
+                nc.vector.quantize_mx(
+                    out=w1_codes[a][:, 256 * g : 256 * (g + 1)].bitcast(FP8X4),
+                    scales=w1_plane[a][:, 256 * g : 256 * (g + 1)],
+                    in_=w1_bf[a][:, 1024 * g : 1024 * (g + 1)],
+                )
 
         def pass_w4(a, h, t):
             cols = slice(h * HALF, (h + 1) * HALF)
@@ -173,61 +156,50 @@ def tile_list_contrast_metric_distance_kernel(
         w4_codes = tile([P, PASSES * H // 2], I32, "w4_codes")
         w4_plane = tile([P, PASSES * H // 4], I32, "w4_plane")
         nc.vector.tensor_copy(
-            w4_codes[:].rearrange("p (t m w) -> p t m w", t=4, w=2),
-            w4_raw[:].rearrange("p (m t w) -> p t m w", t=4, w=2),
+            w4_codes[:].bitcast(U16).rearrange("p (t m) -> p t m", t=4),
+            w4_raw[:].bitcast(U16).rearrange("p (m t) -> p t m", t=4),
         )
         load_tab(2, "slot_d")
         nc.vector.tensor_copy(
-            w4_plane[:].rearrange("p (t m) -> p t m", t=4),
-            w4_scale_rows[:].rearrange("p (m t) -> p t m", t=4),
+            w4_plane[:].bitcast(U8).rearrange("p (t m) -> p t m", t=4),
+            w4_scale_rows[:].bitcast(U8).rearrange("p (m t) -> p t m", t=4),
         )
+        load_w1(2, "slot_e")
 
         for a in range(last):
             if a > 0:
                 picked.append(tile([P, S], U32, "picked%d" % a, "turn%d" % a))
                 for h in range(HALVES):
                     gather(a, h)
-                load_w1(a + 1, "slot_a" if a == 1 else "slot_d")
-            w1_bf.append(tile([P, PACK * H], BF16, "w1_bf%d" % a, "turn%d" % (a + 1)))
-            for t in range(4):
-                dst, src = w1_views(a, t)
-                if a > 0 and t % 2 == 0:
-                    nc.vector.tensor_scalar(dst, src, -1.0, None, ALU.mult)
-                else:
-                    nc.scalar.activation(dst, src, ACT.Copy, scale=-1.0)
-                if t % 2 == 1:
-                    w1_quantize(a, t - 1, t + 1)
             if a == 1:
-                load_tab(last, "slot_b")
-            for one_pass in (pass_w1, pass_w4) if a == 0 else (pass_w4, pass_w1):
-                for h in range(HALVES):
-                    for t in range(4):
-                        one_pass(a, h, t)
+                load_tab(last, "slot_a")
+            w1_bf.append(tile([P, PACK * H], BF16, "w1_bf%d" % a, "turn%d" % (a + 1)))
+            w1_prepare(a)
+            if a == 1:
+                load_w1(last, "slot_b")
+            if a == 0:
+                order = ((pass_w1, 0), (pass_w1, 1), (pass_w4, 0), (pass_w4, 1))
+            else:
+                order = ((pass_w4, 0), (pass_w1, 0), (pass_w1, 1), (pass_w4, 1))
+            for one_pass, h in order:
+                for t in range(4):
+                    one_pass(a, h, t)
 
-        wm_raw = tile([P, PACK, N], F32, "wm_raw", "slot_a")
-        wm_rows = wm.rearrange("(q t b) n -> b q t n", t=4, b=4)
-        for b in range(4):
-            nc.sync.dma_start(wm_raw[b:P:4, :, :], wm_rows[b])
+        wm_raw = tile([P, PACK, N], F32, "wm_raw", "slot_d")
+        nc.sync.dma_start(wm_raw[:], wm.rearrange("(p t) n -> p t n", t=PACK))
 
         picked.append(tile([P, S], U32, "picked%d" % last, "turn%d" % last))
         for h in range(HALVES):
             gather(last, h)
-        w1_bf.append(tile([P, PACK * H], BF16, "w1_bf%d" % last, "slot_b"))
-        for t in range(4):
-            dst, src = w1_views(last, t)
-            if t % 2 == 0:
-                nc.vector.tensor_scalar(dst, src, -1.0, None, ALU.mult)
-            else:
-                nc.scalar.activation(dst, src, ACT.Copy, scale=-1.0)
-                w1_quantize(last, t - 1, t)
-                w1_quantize(last, t, t + 1)
+        w1_bf.append(tile([P, PACK * H], BF16, "w1_bf%d" % last, "slot_a"))
+        w1_prepare(last)
         for h in range(HALVES):
             for t in range(4):
                 pass_w4(last, h, t)
             for t in range(4):
                 pass_w1(last, h, t)
 
-        wm_bf = tile([P, PACK * N], BF16, "wm_bf", "slot_b")
+        wm_bf = tile([P, PACK * N], BF16, "wm_bf", "slot_a")
         wm_codes = tile([P, N], U32, "wm_codes")
         wm_plane = tile([P, N], U8, "wm_plane")
         nc.vector.tensor_copy(
@@ -247,7 +219,7 @@ def tile_list_contrast_metric_distance_kernel(
         h_plane = [tile([P, PART], U8, "h_plane%d" % j) for j in range(PARTS)]
 
         def h_interleave(j):
-            h_bf[j] = tile([P, PACK * PART], BF16, "h_bf%d" % j, "slot_a" if j % 2 == 0 else "slot_b")
+            h_bf[j] = tile([P, PACK * PART], BF16, "h_bf%d" % j, "slot_d" if j % 2 == 0 else "slot_a")
             cols = slice((j % 2) * PART, (j % 2 + 1) * PART)
             nc.vector.tensor_copy(
                 h_bf[j][:].rearrange("p (m i t) -> p m t i", i=4, t=PACK),

@@ -49,26 +49,31 @@ def tile_list_contrast_metric_distance_kernel(
             nc.sync.dma_start(w1_raw[a][:], w1[512 * a : 512 * (a + 1), :].rearrange("(p i) r -> p i r", i=PACK))
 
         gain_sb = tile([P, 4], F32, "gain_sb")
-        c_sb = tile([P, 4], F32, "c_sb")
         nc.sync.dma_start(gain_sb[:], gain.rearrange("(p t) -> p t", t=4))
-        nc.sync.dma_start(c_sb[:], c.rearrange("(p t) -> p t", t=4))
-        load_tab(0, "slot_a")
         offsets = keep.tile([P, S // 16], U16, name="offsets")
         nc.sync.dma_start(offsets[:], offs)
+
+        w4_scale_rows = tile([P, PASSES * H // 4], I32, "w4_scale_rows")
+        nc.vector.memset(w4_scale_rows[:], 0)
+        w4_scales_by_row = w4_scales.rearrange("a (q r) e -> r q a e", r=4)
+        for r in range(4):
+            nc.sync.dma_start(
+                w4_scale_rows[r:P:32, :].rearrange("q (a e) -> q a e", a=PASSES), w4_scales_by_row[r].bitcast(I32)
+            )
 
         tab_scale_rows = tile([P, T // 4], I32, "tab_scale_rows", "slot_b")
         nc.vector.memset(tab_scale_rows[:], 0)
         shifted = [None] + [tile([P, S // 4], I32, "shifted%d" % a) for a in range(1, PASSES)]
-        for q in range(4):
+        for q in (2, 3, 0, 1):
             nc.sync.dma_start(
                 tab_scale_rows[32 * q : 32 * q + 16, :], tab_scales[:, 4 * q : 4 * q + 4, :].bitcast(I32)
             )
         for a in range(1, PASSES):
             nc.vector.memset(shifted[a][96:P, :], 0)
         root0 = tile([P, 4], F32, "root0")
-        inv = tile([P, 4], F32, "inv", "slot_c")
-        quot = tile([P, 4], F32, "quot", "slot_d")
-        both = tile([P, 4], F32, "both", "slot_e")
+        inv = tile([P, 4], F32, "inv", "slot_a")
+        quot = tile([P, 4], F32, "quot", "slot_c")
+        both = tile([P, 4], F32, "both", "slot_d")
         root = tile([P, 4], F32, "root")
         bias = tile([P, 4], F32, "bias")
         nc.scalar.activation(root0[:], gain_sb[:], ACT.Sqrt)
@@ -76,21 +81,16 @@ def tile_list_contrast_metric_distance_kernel(
         nc.vector.tensor_tensor(quot[:], gain_sb[:], inv[:], ALU.mult)
         nc.vector.tensor_tensor(both[:], quot[:], root0[:], ALU.add)
         nc.vector.tensor_scalar(root[:], both[:], 0.5, None, ALU.mult)
-        nc.vector.tensor_tensor(bias[:], root[:], c_sb[:], ALU.mult)
 
+        load_tab(0, "slot_a")
         load_w1(0, "slot_c")
         w4_raw = tile([P, PASSES * H // 2], I32, "w4_raw", "slot_d")
         nc.sync.dma_start(
             w4_raw[:].rearrange("p (a e) -> p a e", a=PASSES), w4_words.rearrange("a p e -> p a e").bitcast(I32)
         )
 
-        w4_scale_rows = tile([P, PASSES * H // 4], I32, "w4_scale_rows", "slot_e")
-        nc.vector.memset(w4_scale_rows[:], 0)
-        w4_scales_by_row = w4_scales.rearrange("a (q r) e -> r q a e", r=4)
-        for r in range(4):
-            nc.sync.dma_start(
-                w4_scale_rows[r:P:32, :].rearrange("q (a e) -> q a e", a=PASSES), w4_scales_by_row[r].bitcast(I32)
-            )
+        c_sb = tile([P, 4], F32, "c_sb", "root0")
+        nc.sync.dma_start(c_sb[:], c.rearrange("(p t) -> p t", t=4))
 
         banks = [[psum.tile([P, HALF], F32, name="bank%d%d" % (h, t)) for t in range(4)] for h in range(HALVES)]
         picked = []
@@ -143,40 +143,39 @@ def tile_list_contrast_metric_distance_kernel(
             )
 
         last = PASSES - 1
-        picked.append(tile([P, S], U32, "picked0"))
-        for h in range(HALVES):
-            gather(0, h)
-        load_tab(1, "slot_a")
+        w4_plane = tile([P, PASSES * H // 4], I32, "w4_plane", "gain_sb")
+        nc.vector.tensor_copy(
+            w4_plane[:].bitcast(U8).rearrange("p (t m) -> p t m", t=4),
+            w4_scale_rows[:].bitcast(U8).rearrange("p (m t) -> p t m", t=4),
+        )
         picked_scales = tile([P, S], U8, "picked_scales")
         nc.vector.tensor_copy(picked_scales[:], tab_scale_rows[:].bitcast(U8).indirect(offsets[:]))
         for a in range(1, PASSES):
             nc.sync.dma_start(shifted[a][0:SHIFT_ROWS, :], picked_scales[4 * a : 4 * a + SHIFT_ROWS, :].bitcast(I32))
 
-        load_w1(1, "slot_b")
+        load_tab(1, "slot_b")
+        picked.append(tile([P, S], U32, "picked0"))
+        for h in range(HALVES):
+            gather(0, h)
+        load_w1(1, "slot_a")
         w4_codes = tile([P, PASSES * H // 2], I32, "w4_codes")
-        w4_plane = tile([P, PASSES * H // 4], I32, "w4_plane")
         nc.vector.tensor_copy(
             w4_codes[:].bitcast(U16).rearrange("p (t m) -> p t m", t=4),
             w4_raw[:].bitcast(U16).rearrange("p (m t) -> p t m", t=4),
         )
         load_tab(2, "slot_d")
-        nc.vector.tensor_copy(
-            w4_plane[:].bitcast(U8).rearrange("p (t m) -> p t m", t=4),
-            w4_scale_rows[:].bitcast(U8).rearrange("p (m t) -> p t m", t=4),
-        )
-        load_w1(2, "slot_e")
+        nc.vector.tensor_tensor(bias[:], root[:], c_sb[:], ALU.mult)
 
         for a in range(last):
             if a > 0:
                 picked.append(tile([P, S], U32, "picked%d" % a, "turn%d" % a))
                 for h in range(HALVES):
                     gather(a, h)
-            if a == 1:
-                load_tab(last, "slot_a")
+                load_w1(a + 1, "slot_b" if a == 1 else "slot_d")
             w1_bf.append(tile([P, PACK * H], BF16, "w1_bf%d" % a, "turn%d" % (a + 1)))
             w1_prepare(a)
             if a == 1:
-                load_w1(last, "slot_b")
+                load_tab(last, "slot_a")
             if a == 0:
                 order = ((pass_w1, 0), (pass_w1, 1), (pass_w4, 0), (pass_w4, 1))
             else:
@@ -185,7 +184,7 @@ def tile_list_contrast_metric_distance_kernel(
                 for t in range(4):
                     one_pass(a, h, t)
 
-        wm_raw = tile([P, PACK, N], F32, "wm_raw", "slot_d")
+        wm_raw = tile([P, PACK, N], F32, "wm_raw", "slot_b")
         nc.sync.dma_start(wm_raw[:], wm.rearrange("(p t) n -> p t n", t=PACK))
 
         picked.append(tile([P, S], U32, "picked%d" % last, "turn%d" % last))
@@ -219,7 +218,7 @@ def tile_list_contrast_metric_distance_kernel(
         h_plane = [tile([P, PART], U8, "h_plane%d" % j) for j in range(PARTS)]
 
         def h_interleave(j):
-            h_bf[j] = tile([P, PACK * PART], BF16, "h_bf%d" % j, "slot_d" if j % 2 == 0 else "slot_a")
+            h_bf[j] = tile([P, PACK * PART], BF16, "h_bf%d" % j, "slot_b" if j % 2 == 0 else "slot_a")
             cols = slice((j % 2) * PART, (j % 2 + 1) * PART)
             nc.vector.tensor_copy(
                 h_bf[j][:].rearrange("p (m i t) -> p m t i", i=4, t=PACK),

@@ -24,6 +24,22 @@ HALVES = S // HALF
 PART = 256
 PARTS = S // PART
 SHIFT_ROWS = 112
+SHARED_FROM = 3
+PLACES = {
+    "c_sb": 0,
+    "tab0": 0,
+    "tab2": 0,
+    "wm_raw": 0,
+    "inv": 16,
+    "w1_raw0": 16,
+    "w1_raw2": 16,
+    "quot": 24,
+    "tab1": 24,
+    "tab3": 24,
+    "tab_scale_rows": 40,
+    "w1_raw1": 40,
+    "w1_raw3": 40,
+}
 
 
 def tile_list_contrast_metric_distance_kernel(
@@ -32,89 +48,100 @@ def tile_list_contrast_metric_distance_kernel(
     nc = tc.nc
     with ExitStack() as ctx:
         keep = ctx.enter_context(tc.tile_pool(name="keep", bufs=1))
+        reuse = ctx.enter_context(tc.tile_pool(name="reuse", bufs=1))
         psum = ctx.enter_context(tc.psum_pool(name="psum", bufs=1))
 
-        def tile(shape, dtype, name, tag=None):
-            return keep.tile(shape, dtype, name=name, tag=tag or name, align_bytes=64)
+        def tile(shape, dtype, name):
+            if name in PLACES:
+                return reuse.tile(shape, dtype, name=name, align_bytes=64, offset=1024 * PLACES[name])
+            return keep.tile(shape, dtype, name=name, align_bytes=64)
 
         tab = {}
         w1_raw = {}
 
-        def load_tab(a, tag):
-            tab[a] = tile([P, T], I32, "tab%d" % a, tag)
+        def load_tab(a):
+            tab[a] = tile([P, T], I32, "tab%d" % a)
             nc.sync.dma_start(tab[a][:], tab_words[a].rearrange("p t i -> p (t i)").bitcast(I32))
 
-        def load_w1(a, tag):
-            w1_raw[a] = tile([P, PACK, H], F32, "w1_raw%d" % a, tag)
+        def load_w1(a):
+            w1_raw[a] = tile([P, PACK, H], F32, "w1_raw%d" % a)
             nc.sync.dma_start(w1_raw[a][:], w1[512 * a : 512 * (a + 1), :].rearrange("(p i) r -> p i r", i=PACK))
 
+        c_sb = tile([P, 4], F32, "c_sb")
+        nc.sync.dma_start(c_sb[:], c.rearrange("(p t) -> p t", t=4))
         gain_sb = tile([P, 4], F32, "gain_sb")
         nc.sync.dma_start(gain_sb[:], gain.rearrange("(p t) -> p t", t=4))
         offsets = keep.tile([P, S // 16], U16, name="offsets")
         nc.sync.dma_start(offsets[:], offs)
+        w4_raw = tile([P, PASSES * H // 2], I32, "w4_raw")
+        nc.sync.dma_start(
+            w4_raw[:].rearrange("p (a e) -> p a e", a=PASSES), w4_words.rearrange("a p e -> p a e").bitcast(I32)
+        )
 
+        tab_scale_rows = tile([P, T // 4], I32, "tab_scale_rows")
         w4_scale_rows = tile([P, PASSES * H // 4], I32, "w4_scale_rows")
+        nc.vector.memset(tab_scale_rows[:], 0)
         nc.vector.memset(w4_scale_rows[:], 0)
+
+        def load_tab_scales(q):
+            nc.sync.dma_start(
+                tab_scale_rows[32 * q : 32 * q + 16, :], tab_scales[:, 4 * q : 4 * q + 4, :].bitcast(I32)
+            )
+
+        for q in (2, 3, 0, 1):
+            load_tab_scales(q)
         w4_scales_by_row = w4_scales.rearrange("a (q r) e -> r q a e", r=4)
         for r in range(4):
             nc.sync.dma_start(
                 w4_scale_rows[r:P:32, :].rearrange("q (a e) -> q a e", a=PASSES), w4_scales_by_row[r].bitcast(I32)
             )
-
-        tab_scale_rows = tile([P, T // 4], I32, "tab_scale_rows", "slot_b")
-        nc.vector.memset(tab_scale_rows[:], 0)
         shifted = [None] + [tile([P, S // 4], I32, "shifted%d" % a) for a in range(1, PASSES)]
-        for q in (2, 3, 0, 1):
-            nc.sync.dma_start(
-                tab_scale_rows[32 * q : 32 * q + 16, :], tab_scales[:, 4 * q : 4 * q + 4, :].bitcast(I32)
-            )
         for a in range(1, PASSES):
             nc.vector.memset(shifted[a][96:P, :], 0)
+
         root0 = tile([P, 4], F32, "root0")
-        inv = tile([P, 4], F32, "inv", "slot_a")
-        quot = tile([P, 4], F32, "quot", "slot_c")
-        both = tile([P, 4], F32, "both", "slot_d")
+        inv = tile([P, 4], F32, "inv")
+        quot = tile([P, 4], F32, "quot")
+        both = tile([P, 4], F32, "both")
         root = tile([P, 4], F32, "root")
         bias = tile([P, 4], F32, "bias")
+        half_c = tile([P, 4], F32, "half_c")
+        nc.vector.tensor_scalar(half_c[:], c_sb[:], 0.5, None, ALU.mult)
         nc.scalar.activation(root0[:], gain_sb[:], ACT.Sqrt)
         nc.vector.reciprocal(inv[:], root0[:])
         nc.vector.tensor_tensor(quot[:], gain_sb[:], inv[:], ALU.mult)
         nc.vector.tensor_tensor(both[:], quot[:], root0[:], ALU.add)
         nc.vector.tensor_scalar(root[:], both[:], 0.5, None, ALU.mult)
-
-        load_tab(0, "slot_a")
-        load_w1(0, "slot_c")
-        w4_raw = tile([P, PASSES * H // 2], I32, "w4_raw", "slot_d")
-        nc.sync.dma_start(
-            w4_raw[:].rearrange("p (a e) -> p a e", a=PASSES), w4_words.rearrange("a p e -> p a e").bitcast(I32)
-        )
-
-        c_sb = tile([P, 4], F32, "c_sb", "root0")
-        nc.sync.dma_start(c_sb[:], c.rearrange("(p t) -> p t", t=4))
+        nc.vector.tensor_tensor(bias[:], both[:], half_c[:], ALU.mult)
+        load_tab(0)
+        load_w1(0)
+        load_tab(1)
 
         banks = [[psum.tile([P, HALF], F32, name="bank%d%d" % (h, t)) for t in range(4)] for h in range(HALVES)]
-        picked = []
-        w1_bf = []
-        w1_codes = [tile([P, H], U32, "w1_codes%d" % a) for a in range(PASSES)]
-        w1_plane = [tile([P, H], U8, "w1_plane%d" % a) for a in range(PASSES)]
+        picked = [[] for a in range(PASSES)]
+        w1_bf = [[tile([P, PACK * H // 2], BF16, "w1_bf%d%d" % (a, g)) for g in range(2)] for a in range(PASSES)]
+        w1_codes = [[tile([P, H // 2], U32, "w1_codes%d%d" % (a, g)) for g in range(2)] for a in range(PASSES)]
+        w1_plane = [[tile([P, H // 2], U8, "w1_plane%d%d" % (a, g)) for g in range(2)] for a in range(PASSES)]
 
-        def gather(a, h):
-            cols = offsets[:, h * (HALF // 16) : (h + 1) * (HALF // 16)]
-            nc.vector.tensor_copy(picked[a][:, h * HALF : (h + 1) * HALF], tab[a][:].bitcast(U32).indirect(cols))
+        def gather(a):
+            for h in range(HALVES):
+                picked[a].append(tile([P, HALF], U32, "picked%d%d" % (a, h)))
+                cols = offsets[:, h * (HALF // 16) : (h + 1) * (HALF // 16)]
+                nc.vector.tensor_copy(picked[a][h][:], tab[a][:].bitcast(U32).indirect(cols))
 
         def w1_prepare(a):
             for g in range(2):
-                dst = w1_bf[a][:, 1024 * g : 1024 * (g + 1)].rearrange("p (t m i) -> p m t i", t=2, i=PACK)
+                dst = w1_bf[a][g][:].rearrange("p (t m i) -> p m t i", t=2, i=PACK)
                 src = w1_raw[a][:].rearrange("p i (m t) -> p m t i", t=4)[:, :, 2 * g : 2 * g + 2, :]
-                if a > 0 and g == 0:
+                if a >= SHARED_FROM and g == 0:
                     nc.vector.tensor_scalar(dst, src, -1.0, None, ALU.mult)
                 else:
                     nc.scalar.activation(dst, src, ACT.Copy, scale=-1.0)
             for g in range(2):
                 nc.vector.quantize_mx(
-                    out=w1_codes[a][:, 256 * g : 256 * (g + 1)].bitcast(FP8X4),
-                    scales=w1_plane[a][:, 256 * g : 256 * (g + 1)],
-                    in_=w1_bf[a][:, 1024 * g : 1024 * (g + 1)],
+                    out=w1_codes[a][g][:].bitcast(FP8X4),
+                    scales=w1_plane[a][g][:],
+                    in_=w1_bf[a][g][:],
                 )
 
         def pass_w4(a, h, t):
@@ -125,80 +152,61 @@ def tile_list_contrast_metric_distance_kernel(
                 out=banks[h][t][:],
                 lhsT=w4_codes[:, col0 // 2 : (col0 + P) // 2].bitcast(FP4X4),
                 lhsT_scale=w4_plane[:, col0 // 4 : (col0 + P) // 4].bitcast(U8),
-                rhs=picked[a][:, h * HALF : (h + 1) * HALF].bitcast(FP8X4),
+                rhs=picked[a][h][:].bitcast(FP8X4),
                 rhs_scale=plane,
-                start=False,
+                start=(a == 0),
                 stop=False,
             )
 
         def pass_w1(a, h, t):
             nc.tensor.matmul_mx(
                 out=banks[h][t][:],
-                lhsT=w1_codes[a][:, P * t : P * (t + 1)].bitcast(FP8X4),
-                lhsT_scale=w1_plane[a][:, P * t : P * (t + 1)],
-                rhs=picked[a][:, h * HALF : (h + 1) * HALF].bitcast(FP8X4),
+                lhsT=w1_codes[a][t // 2][:, P * (t % 2) : P * (t % 2 + 1)].bitcast(FP8X4),
+                lhsT_scale=w1_plane[a][t // 2][:, P * (t % 2) : P * (t % 2 + 1)],
+                rhs=picked[a][h][:].bitcast(FP8X4),
                 rhs_scale=picked_scales[4 * a : P, h * HALF : (h + 1) * HALF],
-                start=(a == 0),
+                start=False,
                 stop=(a == PASSES - 1),
             )
 
-        last = PASSES - 1
-        w4_plane = tile([P, PASSES * H // 4], I32, "w4_plane", "gain_sb")
-        nc.vector.tensor_copy(
-            w4_plane[:].bitcast(U8).rearrange("p (t m) -> p t m", t=4),
-            w4_scale_rows[:].bitcast(U8).rearrange("p (m t) -> p t m", t=4),
-        )
-        picked_scales = tile([P, S], U8, "picked_scales")
-        nc.vector.tensor_copy(picked_scales[:], tab_scale_rows[:].bitcast(U8).indirect(offsets[:]))
-        for a in range(1, PASSES):
-            nc.sync.dma_start(shifted[a][0:SHIFT_ROWS, :], picked_scales[4 * a : 4 * a + SHIFT_ROWS, :].bitcast(I32))
+        def passes(one_pass, a, halves):
+            for h in halves:
+                for t in range(4):
+                    one_pass(a, h, t)
 
-        load_tab(1, "slot_b")
-        picked.append(tile([P, S], U32, "picked0"))
-        for h in range(HALVES):
-            gather(0, h)
-        load_w1(1, "slot_a")
         w4_codes = tile([P, PASSES * H // 2], I32, "w4_codes")
         nc.vector.tensor_copy(
             w4_codes[:].bitcast(U16).rearrange("p (t m) -> p t m", t=4),
             w4_raw[:].bitcast(U16).rearrange("p (m t) -> p t m", t=4),
         )
-        load_tab(2, "slot_d")
-        nc.vector.tensor_tensor(bias[:], root[:], c_sb[:], ALU.mult)
+        picked_scales = tile([P, S], U8, "picked_scales")
+        nc.vector.tensor_copy(picked_scales[:], tab_scale_rows[:].bitcast(U8).indirect(offsets[:]))
+        for a in range(1, PASSES):
+            nc.sync.dma_start(shifted[a][0:SHIFT_ROWS, :], picked_scales[4 * a : 4 * a + SHIFT_ROWS, :].bitcast(I32))
+        load_w1(1)
+        w4_plane = tile([P, PASSES * H // 4], I32, "w4_plane")
+        nc.vector.tensor_copy(
+            w4_plane[:].bitcast(U8).rearrange("p (t m) -> p t m", t=4),
+            w4_scale_rows[:].bitcast(U8).rearrange("p (m t) -> p t m", t=4),
+        )
 
-        for a in range(last):
-            if a > 0:
-                picked.append(tile([P, S], U32, "picked%d" % a, "turn%d" % a))
-                for h in range(HALVES):
-                    gather(a, h)
-                load_w1(a + 1, "slot_b" if a == 1 else "slot_d")
-            w1_bf.append(tile([P, PACK * H], BF16, "w1_bf%d" % a, "turn%d" % (a + 1)))
+        wm_raw = None
+        for a in range(PASSES):
+            gather(a)
+            if a + 2 < PASSES:
+                load_tab(a + 2)
+            if a == 2:
+                wm_raw = tile([P, PACK, N], F32, "wm_raw")
+                nc.sync.dma_start(wm_raw[:], wm.rearrange("(p t) n -> p t n", t=PACK))
+            late = (1,) if 0 < a < PASSES - 1 else ()
+            passes(pass_w4, a, [h for h in range(HALVES) if h not in late])
             w1_prepare(a)
-            if a == 1:
-                load_tab(last, "slot_a")
-            if a == 0:
-                order = ((pass_w1, 0), (pass_w1, 1), (pass_w4, 0), (pass_w4, 1))
-            else:
-                order = ((pass_w4, 0), (pass_w1, 0), (pass_w1, 1), (pass_w4, 1))
-            for one_pass, h in order:
-                for t in range(4):
-                    one_pass(a, h, t)
+            if a + 2 < PASSES:
+                load_w1(a + 2)
+            passes(pass_w1, a, range(HALVES))
+            passes(pass_w4, a, late)
 
-        wm_raw = tile([P, PACK, N], F32, "wm_raw", "slot_b")
-        nc.sync.dma_start(wm_raw[:], wm.rearrange("(p t) n -> p t n", t=PACK))
-
-        picked.append(tile([P, S], U32, "picked%d" % last, "turn%d" % last))
-        for h in range(HALVES):
-            gather(last, h)
-        w1_bf.append(tile([P, PACK * H], BF16, "w1_bf%d" % last, "slot_a"))
-        w1_prepare(last)
-        for h in range(HALVES):
-            for t in range(4):
-                pass_w4(last, h, t)
-            for t in range(4):
-                pass_w1(last, h, t)
-
-        wm_bf = tile([P, PACK * N], BF16, "wm_bf", "slot_a")
+        wm_bf = tile([P, PACK * N], BF16, "wm_bf")
         wm_codes = tile([P, N], U32, "wm_codes")
         wm_plane = tile([P, N], U8, "wm_plane")
         nc.vector.tensor_copy(
@@ -218,7 +226,7 @@ def tile_list_contrast_metric_distance_kernel(
         h_plane = [tile([P, PART], U8, "h_plane%d" % j) for j in range(PARTS)]
 
         def h_interleave(j):
-            h_bf[j] = tile([P, PACK * PART], BF16, "h_bf%d" % j, "slot_b" if j % 2 == 0 else "slot_a")
+            h_bf[j] = tile([P, PACK * PART], BF16, "h_bf%d" % j)
             cols = slice((j % 2) * PART, (j % 2 + 1) * PART)
             nc.vector.tensor_copy(
                 h_bf[j][:].rearrange("p (m i t) -> p m t i", i=4, t=PACK),

@@ -23,22 +23,22 @@ HALF = 512
 HALVES = S // HALF
 PART = 256
 PARTS = S // PART
-SHIFT_ROWS = 112
+ROW0 = 32
+ROW_BYTES = S + H
 SHARED_FROM = 3
 PLACES = {
-    "c_sb": 0,
     "tab0": 0,
-    "tab2": 0,
-    "wm_raw": 0,
-    "inv": 16,
-    "w1_raw0": 16,
-    "w1_raw2": 16,
-    "quot": 24,
-    "tab1": 24,
-    "tab3": 24,
-    "tab_scale_rows": 40,
-    "w1_raw1": 40,
-    "w1_raw3": 40,
+    "w1_raw1": 16,
+    "tab3": 16,
+    "gain_sb": 0,
+    "c_sb": 1,
+    "tab1": 56,
+    "w1_raw2": 56,
+    "wm_raw": 56,
+    "picked_scales": 87,
+    "w4_raw": 88,
+    "tab2": 88,
+    "w1_raw3": 88,
 }
 
 
@@ -53,7 +53,7 @@ def tile_list_contrast_metric_distance_kernel(
 
         def tile(shape, dtype, name):
             if name in PLACES:
-                return reuse.tile(shape, dtype, name=name, align_bytes=64, offset=1024 * PLACES[name])
+                return reuse.tile(shape, dtype, name=name, align_bytes=64, offset=512 * PLACES[name])
             return keep.tile(shape, dtype, name=name, align_bytes=64)
 
         tab = {}
@@ -67,55 +67,18 @@ def tile_list_contrast_metric_distance_kernel(
             w1_raw[a] = tile([P, PACK, H], F32, "w1_raw%d" % a)
             nc.sync.dma_start(w1_raw[a][:], w1[512 * a : 512 * (a + 1), :].rearrange("(p i) r -> p i r", i=PACK))
 
-        c_sb = tile([P, 4], F32, "c_sb")
-        nc.sync.dma_start(c_sb[:], c.rearrange("(p t) -> p t", t=4))
-        gain_sb = tile([P, 4], F32, "gain_sb")
-        nc.sync.dma_start(gain_sb[:], gain.rearrange("(p t) -> p t", t=4))
         offsets = keep.tile([P, S // 16], U16, name="offsets")
         nc.sync.dma_start(offsets[:], offs)
-        w4_raw = tile([P, PASSES * H // 2], I32, "w4_raw")
-        nc.sync.dma_start(
-            w4_raw[:].rearrange("p (a e) -> p a e", a=PASSES), w4_words.rearrange("a p e -> p a e").bitcast(I32)
-        )
-
         tab_scale_rows = tile([P, T // 4], I32, "tab_scale_rows")
-        w4_scale_rows = tile([P, PASSES * H // 4], I32, "w4_scale_rows")
-        nc.vector.memset(tab_scale_rows[:], 0)
-        nc.vector.memset(w4_scale_rows[:], 0)
-
-        def load_tab_scales(q):
-            nc.sync.dma_start(
-                tab_scale_rows[32 * q : 32 * q + 16, :], tab_scales[:, 4 * q : 4 * q + 4, :].bitcast(I32)
-            )
-
-        for q in (2, 3, 0, 1):
-            load_tab_scales(q)
-        w4_scales_by_row = w4_scales.rearrange("a (q r) e -> r q a e", r=4)
-        for r in range(4):
-            nc.sync.dma_start(
-                w4_scale_rows[r:P:32, :].rearrange("q (a e) -> q a e", a=PASSES), w4_scales_by_row[r].bitcast(I32)
-            )
-        shifted = [None] + [tile([P, S // 4], I32, "shifted%d" % a) for a in range(1, PASSES)]
-        for a in range(1, PASSES):
-            nc.vector.memset(shifted[a][96:P, :], 0)
-
-        root0 = tile([P, 4], F32, "root0")
-        inv = tile([P, 4], F32, "inv")
-        quot = tile([P, 4], F32, "quot")
-        both = tile([P, 4], F32, "both")
-        root = tile([P, 4], F32, "root")
-        bias = tile([P, 4], F32, "bias")
-        half_c = tile([P, 4], F32, "half_c")
-        nc.vector.tensor_scalar(half_c[:], c_sb[:], 0.5, None, ALU.mult)
-        nc.scalar.activation(root0[:], gain_sb[:], ACT.Sqrt)
-        nc.vector.reciprocal(inv[:], root0[:])
-        nc.vector.tensor_tensor(quot[:], gain_sb[:], inv[:], ALU.mult)
-        nc.vector.tensor_tensor(both[:], quot[:], root0[:], ALU.add)
-        nc.vector.tensor_scalar(root[:], both[:], 0.5, None, ALU.mult)
-        nc.vector.tensor_tensor(bias[:], both[:], half_c[:], ALU.mult)
+        w4_scale_rows = tile([P, H // 4], I32, "w4_scale_rows")
+        for rows, scales in ((tab_scale_rows, tab_scales), (w4_scale_rows, w4_scales)):
+            nc.vector.memset(rows[0:ROW0, :], 0)
+            nc.vector.memset(rows[ROW0 + 64 : P, :], 0)
+            nc.sync.dma_start(rows[ROW0 : ROW0 + 64, :], scales.rearrange("a q e -> q a e").bitcast(I32))
         load_tab(0)
         load_w1(0)
-        load_tab(1)
+        planes = tile([P, PASSES * ROW_BYTES // 4], I32, "planes")
+        nc.vector.memset(planes[:], 0)
 
         banks = [[psum.tile([P, HALF], F32, name="bank%d%d" % (h, t)) for t in range(4)] for h in range(HALVES)]
         picked = [[] for a in range(PASSES)]
@@ -144,17 +107,18 @@ def tile_list_contrast_metric_distance_kernel(
                     in_=w1_bf[a][g][:],
                 )
 
+        def plane(a, first, width):
+            return planes[:].bitcast(U8)[:, a * ROW_BYTES + first : a * ROW_BYTES + first + width]
+
         def pass_w4(a, h, t):
-            cols = slice(h * HALF, (h + 1) * HALF)
-            plane = picked_scales[:, cols] if a == 0 else shifted[a][:].bitcast(U8)[:, cols]
             col0 = (t * PASSES + a) * P
             nc.tensor.matmul_mx(
                 out=banks[h][t][:],
                 lhsT=w4_codes[:, col0 // 2 : (col0 + P) // 2].bitcast(FP4X4),
-                lhsT_scale=w4_plane[:, col0 // 4 : (col0 + P) // 4].bitcast(U8),
+                lhsT_scale=plane(a, S + t * P, P),
                 rhs=picked[a][h][:].bitcast(FP8X4),
-                rhs_scale=plane,
-                start=(a == 0),
+                rhs_scale=plane(a, h * HALF, HALF),
+                start=False,
                 stop=False,
             )
 
@@ -164,8 +128,8 @@ def tile_list_contrast_metric_distance_kernel(
                 lhsT=w1_codes[a][t // 2][:, P * (t % 2) : P * (t % 2 + 1)].bitcast(FP8X4),
                 lhsT_scale=w1_plane[a][t // 2][:, P * (t % 2) : P * (t % 2 + 1)],
                 rhs=picked[a][h][:].bitcast(FP8X4),
-                rhs_scale=picked_scales[4 * a : P, h * HALF : (h + 1) * HALF],
-                start=False,
+                rhs_scale=plane(a, h * HALF, HALF),
+                start=(a == 0),
                 stop=(a == PASSES - 1),
             )
 
@@ -174,37 +138,70 @@ def tile_list_contrast_metric_distance_kernel(
                 for t in range(4):
                     one_pass(a, h, t)
 
+        scale_rows = tile([P, ROW_BYTES // 4], I32, "scale_rows")
+        picked_scales = tile([P, S], U8, "picked_scales")
+        nc.vector.tensor_copy(picked_scales[:], tab_scale_rows[:].bitcast(U8).indirect(offsets[:]))
+        nc.vector.tensor_copy(
+            scale_rows[:].bitcast(U8)[:, S:ROW_BYTES].rearrange("p (t m) -> p t m", t=4),
+            w4_scale_rows[:].bitcast(U8).rearrange("p (m t) -> p t m", t=4),
+        )
+        nc.vector.tensor_copy(scale_rows[:, 0 : S // 4], picked_scales[:].bitcast(I32))
+        for quadrant in (0, 2, 1, 3):
+            first = ROW0 + 16 * quadrant
+            nc.sync.dma_start(
+                planes[32 * quadrant : 32 * quadrant + 4, :].rearrange("r (a e) -> r a e", a=PASSES),
+                scale_rows[first : first + 16, :],
+            )
+        w4_raw = tile([P, PASSES * H // 2], I32, "w4_raw")
+        nc.sync.dma_start(
+            w4_raw[:].rearrange("p (a e) -> p a e", a=PASSES), w4_words.rearrange("a p e -> p a e").bitcast(I32)
+        )
+        load_tab(1)
+
+        gather(0)
+        load_w1(1)
+        gain_sb = tile([P, 4], F32, "gain_sb")
+        nc.sync.dma_start(gain_sb[:], gain.rearrange("(p t) -> p t", t=4))
+        c_sb = tile([P, 4], F32, "c_sb")
+        nc.sync.dma_start(c_sb[:], c.rearrange("(p t) -> p t", t=4))
+        root0 = tile([P, 4], F32, "root0")
+        inv = tile([P, 4], F32, "inv")
+        quot = tile([P, 4], F32, "quot")
+        both = tile([P, 4], F32, "both")
+        root = tile([P, 4], F32, "root")
+        bias = tile([P, 4], F32, "bias")
+        nc.scalar.activation(root0[:], gain_sb[:], ACT.Sqrt)
+        nc.vector.reciprocal(inv[:], root0[:])
+        nc.vector.tensor_tensor(quot[:], gain_sb[:], inv[:], ALU.mult)
+        nc.vector.tensor_tensor(both[:], quot[:], root0[:], ALU.add)
+        nc.vector.tensor_scalar(root[:], both[:], 0.5, None, ALU.mult)
+        nc.vector.tensor_tensor(bias[:], root[:], c_sb[:], ALU.mult)
+
         w4_codes = tile([P, PASSES * H // 2], I32, "w4_codes")
         nc.vector.tensor_copy(
             w4_codes[:].bitcast(U16).rearrange("p (t m) -> p t m", t=4),
             w4_raw[:].bitcast(U16).rearrange("p (m t) -> p t m", t=4),
         )
-        picked_scales = tile([P, S], U8, "picked_scales")
-        nc.vector.tensor_copy(picked_scales[:], tab_scale_rows[:].bitcast(U8).indirect(offsets[:]))
-        for a in range(1, PASSES):
-            nc.sync.dma_start(shifted[a][0:SHIFT_ROWS, :], picked_scales[4 * a : 4 * a + SHIFT_ROWS, :].bitcast(I32))
-        load_w1(1)
-        w4_plane = tile([P, PASSES * H // 4], I32, "w4_plane")
-        nc.vector.tensor_copy(
-            w4_plane[:].bitcast(U8).rearrange("p (t m) -> p t m", t=4),
-            w4_scale_rows[:].bitcast(U8).rearrange("p (m t) -> p t m", t=4),
-        )
+        load_tab(2)
+        w1_prepare(0)
+        passes(pass_w1, 0, (0, 1))
+        passes(pass_w4, 0, (0, 1))
 
-        wm_raw = None
-        for a in range(PASSES):
+        for a in (1, 2):
             gather(a)
-            if a + 2 < PASSES:
-                load_tab(a + 2)
-            if a == 2:
-                wm_raw = tile([P, PACK, N], F32, "wm_raw")
-                nc.sync.dma_start(wm_raw[:], wm.rearrange("(p t) n -> p t n", t=PACK))
-            late = (1,) if 0 < a < PASSES - 1 else ()
-            passes(pass_w4, a, [h for h in range(HALVES) if h not in late])
+            load_w1(a + 1)
+            passes(pass_w4, a, (0,))
             w1_prepare(a)
-            if a + 2 < PASSES:
-                load_w1(a + 2)
-            passes(pass_w1, a, range(HALVES))
-            passes(pass_w4, a, late)
+            if a == 1:
+                load_tab(3)
+            passes(pass_w1, a, (0, 1))
+            passes(pass_w4, a, (1,))
+        wm_raw = tile([P, PACK, N], F32, "wm_raw")
+        nc.sync.dma_start(wm_raw[:], wm.rearrange("(p t) n -> p t n", t=PACK))
+        gather(3)
+        passes(pass_w4, 3, (0, 1))
+        w1_prepare(3)
+        passes(pass_w1, 3, (0, 1))
 
         wm_bf = tile([P, PACK * N], BF16, "wm_bf")
         wm_codes = tile([P, N], U32, "wm_codes")

@@ -25,20 +25,24 @@ PART = 256
 PARTS = S // PART
 ROW0 = 32
 ROW_BYTES = S + H
-SHARED_FROM = 3
+SHARED_FROM = 1
 PLACES = {
-    "tab0": 0,
-    "w1_raw1": 16,
-    "tab3": 16,
-    "gain_sb": 0,
-    "c_sb": 1,
-    "tab1": 56,
-    "w1_raw2": 56,
-    "wm_raw": 56,
-    "picked_scales": 87,
-    "w4_raw": 88,
-    "tab2": 88,
-    "w1_raw3": 88,
+    "w1_raw0": 48,
+    "w1_raw1": 34,
+    "planes2": 60,
+    "tab2": 63,
+    "w1_raw2": 44,
+    "planes3": 38,
+    "tab3": 4,
+    "w1_raw3": 64,
+    "wm_raw": 44,
+    "tab0": 96,
+    "gain_sb": 96,
+    "c_sb": 97,
+    "planes1": 98,
+    "w4_raw": 128,
+    "picked_scales": 135,
+    "tab1": 136,
 }
 
 
@@ -74,11 +78,21 @@ def tile_list_contrast_metric_distance_kernel(
         for rows, scales in ((tab_scale_rows, tab_scales), (w4_scale_rows, w4_scales)):
             nc.vector.memset(rows[0:ROW0, :], 0)
             nc.vector.memset(rows[ROW0 + 64 : P, :], 0)
-            nc.sync.dma_start(rows[ROW0 : ROW0 + 64, :], scales.rearrange("a q e -> q a e").bitcast(I32))
+            nc.sync.dma_start(rows[ROW0 : ROW0 + 64, :], scales.rearrange("a q e -> (a q) e").bitcast(I32))
         load_tab(0)
         load_w1(0)
-        planes = tile([P, PASSES * ROW_BYTES // 4], I32, "planes")
-        nc.vector.memset(planes[:], 0)
+        planes = {}
+
+        def clear_planes(a):
+            planes[a] = tile([P, ROW_BYTES // 4], I32, "planes%d" % a)
+            nc.vector.memset(planes[a][:], 0)
+
+        def move_scale_rows(a):
+            first = ROW0 + 16 * a
+            for r in range(4):
+                nc.sync.dma_start(planes[a][r:P:32, :], scale_rows[first + r : first + 16 : 4, :])
+
+        clear_planes(0)
 
         banks = [[psum.tile([P, HALF], F32, name="bank%d%d" % (h, t)) for t in range(4)] for h in range(HALVES)]
         picked = [[] for a in range(PASSES)]
@@ -108,7 +122,7 @@ def tile_list_contrast_metric_distance_kernel(
                 )
 
         def plane(a, first, width):
-            return planes[:].bitcast(U8)[:, a * ROW_BYTES + first : a * ROW_BYTES + first + width]
+            return planes[a][:].bitcast(U8)[:, first : first + width]
 
         def pass_w4(a, h, t):
             col0 = (t * PASSES + a) * P
@@ -146,12 +160,7 @@ def tile_list_contrast_metric_distance_kernel(
             w4_scale_rows[:].bitcast(U8).rearrange("p (m t) -> p t m", t=4),
         )
         nc.vector.tensor_copy(scale_rows[:, 0 : S // 4], picked_scales[:].bitcast(I32))
-        for quadrant in (0, 2, 1, 3):
-            first = ROW0 + 16 * quadrant
-            nc.sync.dma_start(
-                planes[32 * quadrant : 32 * quadrant + 4, :].rearrange("r (a e) -> r a e", a=PASSES),
-                scale_rows[first : first + 16, :],
-            )
+        move_scale_rows(0)
         w4_raw = tile([P, PASSES * H // 2], I32, "w4_raw")
         nc.sync.dma_start(
             w4_raw[:].rearrange("p (a e) -> p a e", a=PASSES), w4_words.rearrange("a p e -> p a e").bitcast(I32)
@@ -159,11 +168,12 @@ def tile_list_contrast_metric_distance_kernel(
         load_tab(1)
 
         gather(0)
-        load_w1(1)
         gain_sb = tile([P, 4], F32, "gain_sb")
         nc.sync.dma_start(gain_sb[:], gain.rearrange("(p t) -> p t", t=4))
         c_sb = tile([P, 4], F32, "c_sb")
         nc.sync.dma_start(c_sb[:], c.rearrange("(p t) -> p t", t=4))
+        clear_planes(1)
+        move_scale_rows(1)
         root0 = tile([P, 4], F32, "root0")
         inv = tile([P, 4], F32, "inv")
         quot = tile([P, 4], F32, "quot")
@@ -182,26 +192,24 @@ def tile_list_contrast_metric_distance_kernel(
             w4_codes[:].bitcast(U16).rearrange("p (t m) -> p t m", t=4),
             w4_raw[:].bitcast(U16).rearrange("p (m t) -> p t m", t=4),
         )
-        load_tab(2)
-        w1_prepare(0)
-        passes(pass_w1, 0, (0, 1))
-        passes(pass_w4, 0, (0, 1))
 
-        for a in (1, 2):
-            gather(a)
-            load_w1(a + 1)
-            passes(pass_w4, a, (0,))
+        for a in range(PASSES):
+            if a > 0:
+                gather(a)
+                if a == 2:
+                    load_w1(3)
+                passes(pass_w4, a, (0,) if a < 3 else (0, 1))
             w1_prepare(a)
-            if a == 1:
-                load_tab(3)
+            if a < 2:
+                load_w1(a + 1)
+                load_tab(a + 2)
+                clear_planes(a + 2)
+                move_scale_rows(a + 2)
+            if a == 2:
+                wm_raw = tile([P, PACK, N], F32, "wm_raw")
+                nc.sync.dma_start(wm_raw[:], wm.rearrange("(p t) n -> p t n", t=PACK))
             passes(pass_w1, a, (0, 1))
-            passes(pass_w4, a, (1,))
-        wm_raw = tile([P, PACK, N], F32, "wm_raw")
-        nc.sync.dma_start(wm_raw[:], wm.rearrange("(p t) n -> p t n", t=PACK))
-        gather(3)
-        passes(pass_w4, 3, (0, 1))
-        w1_prepare(3)
-        passes(pass_w1, 3, (0, 1))
+            passes(pass_w4, a, ((0, 1), (1,), (1,), ())[a])
 
         wm_bf = tile([P, PACK * N], BF16, "wm_bf")
         wm_codes = tile([P, N], U32, "wm_codes")

@@ -26,6 +26,7 @@ PARTS = S // PART
 ROW0 = 32
 ROW_BYTES = S + H
 SHARED_FROM = 1
+LAST = PASSES - 1
 PLACES = {
     "w1_raw0": 48,
     "w1_raw1": 34,
@@ -34,7 +35,8 @@ PLACES = {
     "w1_raw2": 44,
     "planes3": 38,
     "tab3": 4,
-    "w1_raw3": 64,
+    "w1_last0": 64,
+    "w1_last1": 72,
     "wm_raw": 44,
     "tab0": 96,
     "gain_sb": 96,
@@ -43,6 +45,9 @@ PLACES = {
     "w4_raw": 128,
     "picked_scales": 135,
     "tab1": 136,
+    "wm_bf": 168,
+    "h_bf0": 168,
+    "h_bf1": 172,
 }
 
 
@@ -70,6 +75,14 @@ def tile_list_contrast_metric_distance_kernel(
         def load_w1(a):
             w1_raw[a] = tile([P, PACK, H], F32, "w1_raw%d" % a)
             nc.sync.dma_start(w1_raw[a][:], w1[512 * a : 512 * (a + 1), :].rearrange("(p i) r -> p i r", i=PACK))
+
+        w1_last = {}
+
+        def load_w1_last():
+            rows = w1[512 * LAST : 512 * (LAST + 1), :].rearrange("(p i) r -> p i r", i=PACK)
+            for e in range(2):
+                w1_last[e] = tile([P, 2, H], F32, "w1_last%d" % e)
+                nc.sync.dma_start(w1_last[e][:], rows[:, 2 * e : 2 * e + 2, :])
 
         offsets = keep.tile([P, S // 16], U16, name="offsets")
         nc.sync.dma_start(offsets[:], offs)
@@ -121,10 +134,26 @@ def tile_list_contrast_metric_distance_kernel(
                     in_=w1_bf[a][g][:],
                 )
 
+        def w1_prepare_last():
+            for e in range(2):
+                for g in range(2):
+                    dst = w1_bf[LAST][g][:].rearrange("p (t m i) -> p m t i", t=2, i=PACK)[:, :, :, 2 * e : 2 * e + 2]
+                    src = w1_last[e][:].rearrange("p i (m t) -> p m t i", t=4)[:, :, 2 * g : 2 * g + 2, :]
+                    if e == 0:
+                        nc.scalar.activation(dst, src, ACT.Copy, scale=-1.0)
+                    else:
+                        nc.vector.tensor_scalar(dst, src, -1.0, None, ALU.mult)
+                        for t in range(2):
+                            nc.vector.quantize_mx(
+                                out=w1_codes[LAST][g][:, P * t : P * (t + 1)].bitcast(FP8X4),
+                                scales=w1_plane[LAST][g][:, P * t : P * (t + 1)],
+                                in_=w1_bf[LAST][g][:, PACK * P * t : PACK * P * (t + 1)],
+                            )
+
         def plane(a, first, width):
             return planes[a][:].bitcast(U8)[:, first : first + width]
 
-        def pass_w4(a, h, t):
+        def pass_w4(a, h, t, stop=False):
             col0 = (t * PASSES + a) * P
             nc.tensor.matmul_mx(
                 out=banks[h][t][:],
@@ -133,10 +162,10 @@ def tile_list_contrast_metric_distance_kernel(
                 rhs=picked[a][h][:].bitcast(FP8X4),
                 rhs_scale=plane(a, h * HALF, HALF),
                 start=False,
-                stop=False,
+                stop=stop,
             )
 
-        def pass_w1(a, h, t):
+        def pass_w1(a, h, t, stop=False):
             nc.tensor.matmul_mx(
                 out=banks[h][t][:],
                 lhsT=w1_codes[a][t // 2][:, P * (t % 2) : P * (t % 2 + 1)].bitcast(FP8X4),
@@ -144,7 +173,7 @@ def tile_list_contrast_metric_distance_kernel(
                 rhs=picked[a][h][:].bitcast(FP8X4),
                 rhs_scale=plane(a, h * HALF, HALF),
                 start=(a == 0),
-                stop=(a == PASSES - 1),
+                stop=stop,
             )
 
         def passes(one_pass, a, halves):
@@ -193,12 +222,12 @@ def tile_list_contrast_metric_distance_kernel(
             w4_raw[:].bitcast(U16).rearrange("p (m t) -> p t m", t=4),
         )
 
-        for a in range(PASSES):
+        for a in range(LAST):
             if a > 0:
                 gather(a)
                 if a == 2:
-                    load_w1(3)
-                passes(pass_w4, a, (0,) if a < 3 else (0, 1))
+                    load_w1_last()
+                passes(pass_w4, a, (0,))
             w1_prepare(a)
             if a < 2:
                 load_w1(a + 1)
@@ -209,7 +238,19 @@ def tile_list_contrast_metric_distance_kernel(
                 wm_raw = tile([P, PACK, N], F32, "wm_raw")
                 nc.sync.dma_start(wm_raw[:], wm.rearrange("(p t) n -> p t n", t=PACK))
             passes(pass_w1, a, (0, 1))
-            passes(pass_w4, a, ((0, 1), (1,), (1,), ())[a])
+            passes(pass_w4, a, (0, 1) if a == 0 else (1,))
+
+        gather(LAST)
+        passes(pass_w4, LAST, (0,))
+        for t in range(2):
+            pass_w4(LAST, 1, t)
+        w1_prepare_last()
+        for t in range(4):
+            pass_w1(LAST, 0, t, stop=True)
+        for t in range(4):
+            pass_w1(LAST, 1, t, stop=t < 2)
+            if t >= 2:
+                pass_w4(LAST, 1, t, stop=True)
 
         wm_bf = tile([P, PACK * N], BF16, "wm_bf")
         wm_codes = tile([P, N], U32, "wm_codes")
@@ -219,52 +260,57 @@ def tile_list_contrast_metric_distance_kernel(
             wm_raw[:].rearrange("p t (m j) -> p m t j", j=4),
         )
 
-        h_rows = [tile([P, PACK, HALF], BF16, "h_rows%d" % h) for h in range(HALVES)]
-        for h in range(HALVES):
+        nc.vector.quantize_mx(out=wm_codes[:].bitcast(FP8X4), scales=wm_plane[:], in_=wm_bf[:])
+
+        def square(rows, h, cols):
             for t in range(4):
                 nc.scalar.activation(
-                    h_rows[h][:, t, :], banks[h][t][:], ACT.Square, bias=bias[:, t : t + 1], scale=root[:, t : t + 1]
+                    rows[:, t, :], banks[h][t][:, cols], ACT.Square, bias=bias[:, t : t + 1], scale=root[:, t : t + 1]
                 )
 
-        h_bf = {}
+        first_rows = tile([P, PACK, HALF], BF16, "first_rows")
+        square(first_rows, 0, slice(0, HALF))
+        h_rows = [first_rows[:, :, 0:PART], first_rows[:, :, PART:HALF]]
+        for j in range(2, PARTS):
+            rows = tile([P, PACK, PART], BF16, "rows%d" % j)
+            square(rows, 1, slice((j - 2) * PART, (j - 1) * PART))
+            h_rows.append(rows[:])
+
         h_codes = [tile([P, PART], U32, "h_codes%d" % j) for j in range(PARTS)]
         h_plane = [tile([P, PART], U8, "h_plane%d" % j) for j in range(PARTS)]
-
-        def h_interleave(j):
-            h_bf[j] = tile([P, PACK * PART], BF16, "h_bf%d" % j)
-            cols = slice((j % 2) * PART, (j % 2 + 1) * PART)
+        for j in range(PARTS):
+            h_bf = tile([P, PACK * PART], BF16, "h_bf%d" % j)
             nc.vector.tensor_copy(
-                h_bf[j][:].rearrange("p (m i t) -> p m t i", i=4, t=PACK),
-                h_rows[j // 2][:, :, cols].rearrange("p t (m i) -> p m t i", i=4),
+                h_bf[:].rearrange("p (m i t) -> p m t i", i=4, t=PACK),
+                h_rows[j].rearrange("p t (m i) -> p m t i", i=4),
+            )
+            nc.vector.quantize_mx(out=h_codes[j][:].bitcast(FP8X4), scales=h_plane[j][:], in_=h_bf[:])
+
+        def metric_product(acc, u, j):
+            nc.tensor.matmul_mx(
+                out=acc,
+                lhsT=wm_codes[:, P * u : P * (u + 1)].bitcast(FP8X4),
+                lhsT_scale=wm_plane[:, P * u : P * (u + 1)],
+                rhs=h_codes[j][:].bitcast(FP8X4),
+                rhs_scale=h_plane[j][:],
+                start=True,
+                stop=True,
             )
 
-        def h_quantize(j):
-            nc.vector.quantize_mx(out=h_codes[j][:].bitcast(FP8X4), scales=h_plane[j][:], in_=h_bf[j][:])
-
-        h_interleave(0)
-        nc.vector.quantize_mx(out=wm_codes[:].bitcast(FP8X4), scales=wm_plane[:], in_=wm_bf[:])
-        h_quantize(0)
-        h_interleave(1)
-        for j in range(1, PARTS):
-            if j + 1 < PARTS:
-                h_interleave(j + 1)
-            h_quantize(j)
-
         out_rows = out.rearrange("(u p) j -> p u j", p=P)
-        for j in range(PARTS):
+        for j in range(2):
             for pair in range(2):
-                acc = psum.tile([P, 2, PART], F32, name="bank%d%d" % (j // 2, 2 * (j % 2) + pair))
+                acc = psum.tile([P, 2, PART], F32, name="bank0%d" % (2 * j + pair))
                 for e in range(2):
-                    u = 2 * pair + e
-                    nc.tensor.matmul_mx(
-                        out=acc[:, e, :],
-                        lhsT=wm_codes[:, P * u : P * (u + 1)].bitcast(FP8X4),
-                        lhsT_scale=wm_plane[:, P * u : P * (u + 1)],
-                        rhs=h_codes[j][:].bitcast(FP8X4),
-                        rhs_scale=h_plane[j][:],
-                        start=True,
-                        stop=True,
-                    )
+                    metric_product(acc[:, e, :], 2 * pair + e, j)
                 dist = tile([P, 2, PART], F32, "dist%d%d" % (j, pair))
                 nc.scalar.activation(dist[:], acc[:], ACT.Sqrt)
                 nc.sync.dma_start(out_rows[:, 2 * pair : 2 * pair + 2, j * PART : (j + 1) * PART], dist[:])
+        accs = [psum.tile([P, HALF], F32, name="bank1%d" % u) for u in range(4)]
+        for j in range(2, PARTS):
+            for u in range(4):
+                metric_product(accs[u][:, (j - 2) * PART : (j - 1) * PART], u, j)
+        for u in range(4):
+            dist = tile([P, HALF], F32, "dist_last%d" % u)
+            nc.scalar.activation(dist[:], accs[u][:], ACT.Sqrt)
+            nc.sync.dma_start(out_rows[:, u, HALF:S], dist[:])

@@ -33,7 +33,7 @@ PLACES = {
     "planes2": 60,
     "tab2": 63,
     "w1_raw2": 44,
-    "planes3": 38,
+    "planes3": 80,
     "tab3": 4,
     "w1_last0": 64,
     "w1_last1": 72,
@@ -227,30 +227,35 @@ def tile_list_contrast_metric_distance_kernel(
                 gather(a)
                 if a == 2:
                     load_w1_last()
-                passes(pass_w4, a, (0,))
+                    clear_planes(LAST)
+                    move_scale_rows(LAST)
+                for t in range(4 if a < 2 else 2):
+                    pass_w4(a, 0, t)
             w1_prepare(a)
             if a < 2:
                 load_w1(a + 1)
                 load_tab(a + 2)
-                clear_planes(a + 2)
-                move_scale_rows(a + 2)
+            if a == 0:
+                clear_planes(2)
+                move_scale_rows(2)
             if a == 2:
                 wm_raw = tile([P, PACK, N], F32, "wm_raw")
                 nc.sync.dma_start(wm_raw[:], wm.rearrange("(p t) n -> p t n", t=PACK))
             passes(pass_w1, a, (0, 1))
+            if a == 2:
+                for t in range(2, 4):
+                    pass_w4(a, 0, t)
             passes(pass_w4, a, (0, 1) if a == 0 else (1,))
 
         gather(LAST)
-        passes(pass_w4, LAST, (0,))
         for t in range(2):
-            pass_w4(LAST, 1, t)
+            pass_w4(LAST, 0, t)
         w1_prepare_last()
-        for t in range(4):
+        for t in range(2):
             pass_w1(LAST, 0, t, stop=True)
-        for t in range(4):
-            pass_w1(LAST, 1, t, stop=t < 2)
-            if t >= 2:
-                pass_w4(LAST, 1, t, stop=True)
+        for h, t in [(0, 2), (0, 3)] + [(1, t) for t in range(4)]:
+            pass_w1(LAST, h, t)
+            pass_w4(LAST, h, t, stop=True)
 
         wm_bf = tile([P, PACK * N], BF16, "wm_bf")
         wm_codes = tile([P, N], U32, "wm_codes")
@@ -262,29 +267,30 @@ def tile_list_contrast_metric_distance_kernel(
 
         nc.vector.quantize_mx(out=wm_codes[:].bitcast(FP8X4), scales=wm_plane[:], in_=wm_bf[:])
 
-        def square(rows, h, cols):
-            for t in range(4):
-                nc.scalar.activation(
-                    rows[:, t, :], banks[h][t][:, cols], ACT.Square, bias=bias[:, t : t + 1], scale=root[:, t : t + 1]
-                )
+        def square(rows, h, t, cols):
+            nc.scalar.activation(
+                rows[:, t, cols], banks[h][t][:, cols], ACT.Square, bias=bias[:, t : t + 1], scale=root[:, t : t + 1]
+            )
 
-        first_rows = tile([P, PACK, HALF], BF16, "first_rows")
-        square(first_rows, 0, slice(0, HALF))
-        h_rows = [first_rows[:, :, 0:PART], first_rows[:, :, PART:HALF]]
-        for j in range(2, PARTS):
-            rows = tile([P, PACK, PART], BF16, "rows%d" % j)
-            square(rows, 1, slice((j - 2) * PART, (j - 1) * PART))
-            h_rows.append(rows[:])
+        rows = [tile([P, PACK, HALF], BF16, "rows%d" % h) for h in range(HALVES)]
+        for h, t in [(0, t) for t in range(4)] + [(1, 0), (1, 1)]:
+            square(rows[h], h, t, slice(0, HALF))
+        for j in range(2):
+            for t in range(2, 4):
+                square(rows[1], 1, t, slice(j * PART, (j + 1) * PART))
+        h_rows = [rows[j // 2][:, :, (j % 2) * PART : (j % 2 + 1) * PART] for j in range(PARTS)]
 
         h_codes = [tile([P, PART], U32, "h_codes%d" % j) for j in range(PARTS)]
         h_plane = [tile([P, PART], U8, "h_plane%d" % j) for j in range(PARTS)]
-        for j in range(PARTS):
-            h_bf = tile([P, PACK * PART], BF16, "h_bf%d" % j)
-            nc.vector.tensor_copy(
-                h_bf[:].rearrange("p (m i t) -> p m t i", i=4, t=PACK),
-                h_rows[j].rearrange("p t (m i) -> p m t i", i=4),
-            )
-            nc.vector.quantize_mx(out=h_codes[j][:].bitcast(FP8X4), scales=h_plane[j][:], in_=h_bf[:])
+        h_bf = [tile([P, PACK * PART], BF16, "h_bf%d" % j) for j in range(PARTS)]
+        for h in range(HALVES):
+            for j in (2 * h, 2 * h + 1):
+                nc.vector.tensor_copy(
+                    h_bf[j][:].rearrange("p (m i t) -> p m t i", i=4, t=PACK),
+                    h_rows[j].rearrange("p t (m i) -> p m t i", i=4),
+                )
+            for j in (2 * h, 2 * h + 1):
+                nc.vector.quantize_mx(out=h_codes[j][:].bitcast(FP8X4), scales=h_plane[j][:], in_=h_bf[j][:])
 
         def metric_product(acc, u, j):
             nc.tensor.matmul_mx(

@@ -45,8 +45,8 @@ PLACES = {
     "w4_raw": 128,
     "picked_scales": 135,
     "tab1": 136,
-    "wm_bf": 168,
-    "h_bf0": 168,
+    "wm_bf0": 168,
+    "wm_bf1": 172,
     "h_bf1": 172,
 }
 
@@ -248,24 +248,28 @@ def tile_list_contrast_metric_distance_kernel(
             passes(pass_w4, a, (0, 1) if a == 0 else (1,))
 
         gather(LAST)
-        for t in range(2):
+        for t in range(3):
             pass_w4(LAST, 0, t)
         w1_prepare_last()
-        for t in range(2):
+        for t in range(3):
             pass_w1(LAST, 0, t, stop=True)
-        for h, t in [(0, 2), (0, 3)] + [(1, t) for t in range(4)]:
+        for h, t in [(0, 3)] + [(1, t) for t in range(4)]:
             pass_w1(LAST, h, t)
             pass_w4(LAST, h, t, stop=True)
 
-        wm_bf = tile([P, PACK * N], BF16, "wm_bf")
-        wm_codes = tile([P, N], U32, "wm_codes")
-        wm_plane = tile([P, N], U8, "wm_plane")
-        nc.vector.tensor_copy(
-            wm_bf[:].rearrange("p (m j t) -> p m t j", j=4, t=PACK),
-            wm_raw[:].rearrange("p t (m j) -> p m t j", j=4),
-        )
+        wm_bf = [tile([P, PACK * N // 2], BF16, "wm_bf%d" % g) for g in range(2)]
+        wm_codes = [tile([P, N // 2], U32, "wm_codes%d" % g) for g in range(2)]
+        wm_plane = [tile([P, N // 2], U8, "wm_plane%d" % g) for g in range(2)]
+        for g in range(2):
+            nc.vector.tensor_copy(
+                wm_bf[g][:].rearrange("p (m j t) -> p m t j", j=4, t=PACK),
+                wm_raw[:, :, g * (N // 2) : (g + 1) * (N // 2)].rearrange("p t (m j) -> p m t j", j=4),
+            )
 
-        nc.vector.quantize_mx(out=wm_codes[:].bitcast(FP8X4), scales=wm_plane[:], in_=wm_bf[:])
+        def wm_quantise(g):
+            nc.vector.quantize_mx(out=wm_codes[g][:].bitcast(FP8X4), scales=wm_plane[g][:], in_=wm_bf[g][:])
+
+        wm_quantise(0)
 
         def square(rows, h, t, cols):
             nc.scalar.activation(
@@ -273,50 +277,71 @@ def tile_list_contrast_metric_distance_kernel(
             )
 
         rows = [tile([P, PACK, HALF], BF16, "rows%d" % h) for h in range(HALVES)]
-        for h, t in [(0, t) for t in range(4)] + [(1, 0), (1, 1)]:
-            square(rows[h], h, t, slice(0, HALF))
-        for j in range(2):
-            for t in range(2, 4):
-                square(rows[1], 1, t, slice(j * PART, (j + 1) * PART))
         h_rows = [rows[j // 2][:, :, (j % 2) * PART : (j % 2 + 1) * PART] for j in range(PARTS)]
-
         h_codes = [tile([P, PART], U32, "h_codes%d" % j) for j in range(PARTS)]
         h_plane = [tile([P, PART], U8, "h_plane%d" % j) for j in range(PARTS)]
         h_bf = [tile([P, PACK * PART], BF16, "h_bf%d" % j) for j in range(PARTS)]
-        for h in range(HALVES):
-            for j in (2 * h, 2 * h + 1):
-                nc.vector.tensor_copy(
-                    h_bf[j][:].rearrange("p (m i t) -> p m t i", i=4, t=PACK),
-                    h_rows[j].rearrange("p t (m i) -> p m t i", i=4),
-                )
-            for j in (2 * h, 2 * h + 1):
-                nc.vector.quantize_mx(out=h_codes[j][:].bitcast(FP8X4), scales=h_plane[j][:], in_=h_bf[j][:])
+        out_rows = out.rearrange("(u p) j -> p u j", p=P)
+
+        def square_whole(h):
+            for t in range(2):
+                square(rows[h], h, t, slice(0, HALF))
+
+        def square_part(j):
+            for t in range(2, 4):
+                square(rows[j // 2], j // 2, t, slice((j % 2) * PART, (j % 2 + 1) * PART))
+
+        def h_copy(j):
+            nc.vector.tensor_copy(
+                h_bf[j][:].rearrange("p (m i t) -> p m t i", i=4, t=PACK),
+                h_rows[j].rearrange("p t (m i) -> p m t i", i=4),
+            )
+
+        def h_quantise(j):
+            nc.vector.quantize_mx(out=h_codes[j][:].bitcast(FP8X4), scales=h_plane[j][:], in_=h_bf[j][:])
 
         def metric_product(acc, u, j):
             nc.tensor.matmul_mx(
                 out=acc,
-                lhsT=wm_codes[:, P * u : P * (u + 1)].bitcast(FP8X4),
-                lhsT_scale=wm_plane[:, P * u : P * (u + 1)],
+                lhsT=wm_codes[u // 2][:, P * (u % 2) : P * (u % 2 + 1)].bitcast(FP8X4),
+                lhsT_scale=wm_plane[u // 2][:, P * (u % 2) : P * (u % 2 + 1)],
                 rhs=h_codes[j][:].bitcast(FP8X4),
                 rhs_scale=h_plane[j][:],
                 start=True,
                 stop=True,
             )
 
-        out_rows = out.rearrange("(u p) j -> p u j", p=P)
-        for j in range(2):
+        def finish_part(j, names):
             for pair in range(2):
-                acc = psum.tile([P, 2, PART], F32, name="bank0%d" % (2 * j + pair))
+                acc = psum.tile([P, 2, PART], F32, name=names[pair])
                 for e in range(2):
                     metric_product(acc[:, e, :], 2 * pair + e, j)
                 dist = tile([P, 2, PART], F32, "dist%d%d" % (j, pair))
                 nc.scalar.activation(dist[:], acc[:], ACT.Sqrt)
                 nc.sync.dma_start(out_rows[:, 2 * pair : 2 * pair + 2, j * PART : (j + 1) * PART], dist[:])
-        accs = [psum.tile([P, HALF], F32, name="bank1%d" % u) for u in range(4)]
-        for j in range(2, PARTS):
+
+        square_whole(0)
+        square_part(0)
+        square_part(1)
+        square_whole(1)
+        square_part(2)
+        h_copy(0)
+        wm_quantise(1)
+        h_quantise(0)
+        finish_part(0, ("bank00", "bank01"))
+        square_part(3)
+        h_copy(1)
+        h_copy(2)
+        h_quantise(1)
+        h_quantise(2)
+        accs = [psum.tile([P, HALF], F32, name=name) for name in ("bank02", "bank03", "bank10", "bank11")]
+        for j in (1, 2):
             for u in range(4):
-                metric_product(accs[u][:, (j - 2) * PART : (j - 1) * PART], u, j)
+                metric_product(accs[u][:, (j - 1) * PART : j * PART], u, j)
         for u in range(4):
-            dist = tile([P, HALF], F32, "dist_last%d" % u)
+            dist = tile([P, HALF], F32, "dist_mid%d" % u)
             nc.scalar.activation(dist[:], accs[u][:], ACT.Sqrt)
-            nc.sync.dma_start(out_rows[:, u, HALF:S], dist[:])
+            nc.sync.dma_start(out_rows[:, u, PART : 3 * PART], dist[:])
+        h_copy(3)
+        h_quantise(3)
+        finish_part(3, ("bank12", "bank13"))

@@ -37,7 +37,9 @@ PLACES = {
     "tab3": 4,
     "w1_last0": 64,
     "w1_last1": 72,
-    "wm_raw": 44,
+    "wm_raw0": 44,
+    "wm_raw1": 52,
+    "w1_bf31": 170,
     "tab0": 96,
     "gain_sb": 96,
     "c_sb": 97,
@@ -123,7 +125,7 @@ def tile_list_contrast_metric_distance_kernel(
             for g in range(2):
                 dst = w1_bf[a][g][:].rearrange("p (t m i) -> p m t i", t=2, i=PACK)
                 src = w1_raw[a][:].rearrange("p i (m t) -> p m t i", t=4)[:, :, 2 * g : 2 * g + 2, :]
-                if a >= SHARED_FROM and g == 0:
+                if a == SHARED_FROM and g == 0:
                     nc.vector.tensor_scalar(dst, src, -1.0, None, ALU.mult)
                 else:
                     nc.scalar.activation(dst, src, ACT.Copy, scale=-1.0)
@@ -134,21 +136,32 @@ def tile_list_contrast_metric_distance_kernel(
                     in_=w1_bf[a][g][:],
                 )
 
+        def w1_last_views(e, g):
+            dst = w1_bf[LAST][g][:].rearrange("p (t m i) -> p m t i", t=2, i=PACK)[:, :, :, 2 * e : 2 * e + 2]
+            src = w1_last[e][:].rearrange("p i (m t) -> p m t i", t=4)[:, :, 2 * g : 2 * g + 2, :]
+            return dst, src
+
+        def w1_last_quantise(t):
+            g, col0 = t // 2, P * (t % 2)
+            nc.vector.quantize_mx(
+                out=w1_codes[LAST][g][:, col0 : col0 + P].bitcast(FP8X4),
+                scales=w1_plane[LAST][g][:, col0 : col0 + P],
+                in_=w1_bf[LAST][g][:, PACK * col0 : PACK * (col0 + P)],
+            )
+
         def w1_prepare_last():
-            for e in range(2):
-                for g in range(2):
-                    dst = w1_bf[LAST][g][:].rearrange("p (t m i) -> p m t i", t=2, i=PACK)[:, :, :, 2 * e : 2 * e + 2]
-                    src = w1_last[e][:].rearrange("p i (m t) -> p m t i", t=4)[:, :, 2 * g : 2 * g + 2, :]
-                    if e == 0:
-                        nc.scalar.activation(dst, src, ACT.Copy, scale=-1.0)
-                    else:
-                        nc.vector.tensor_scalar(dst, src, -1.0, None, ALU.mult)
-                        for t in range(2):
-                            nc.vector.quantize_mx(
-                                out=w1_codes[LAST][g][:, P * t : P * (t + 1)].bitcast(FP8X4),
-                                scales=w1_plane[LAST][g][:, P * t : P * (t + 1)],
-                                in_=w1_bf[LAST][g][:, PACK * P * t : PACK * P * (t + 1)],
-                            )
+            for g in range(2):
+                dst, src = w1_last_views(0, g)
+                nc.scalar.activation(dst, src, ACT.Copy, scale=-1.0)
+            dst, src = w1_last_views(1, 0)
+            nc.vector.tensor_scalar(dst, src, -1.0, None, ALU.mult)
+            dst, src = w1_last_views(1, 1)
+            for t in range(2):
+                columns = slice(t * P // 2, (t + 1) * P // 2)
+                nc.vector.tensor_scalar(dst[:, columns], src[:, columns], -1.0, None, ALU.mult)
+                w1_last_quantise(t)
+            for t in range(2, 4):
+                w1_last_quantise(t)
 
         def plane(a, first, width):
             return planes[a][:].bitcast(U8)[:, first : first + width]
@@ -229,8 +242,8 @@ def tile_list_contrast_metric_distance_kernel(
                     load_w1_last()
                     clear_planes(LAST)
                     move_scale_rows(LAST)
-                for t in range(4 if a < 2 else 2):
-                    pass_w4(a, 0, t)
+                for h, t in [(0, t) for t in range(4)] if a < 2 else [(0, 0), (0, 1), (1, 0), (1, 1)]:
+                    pass_w4(a, h, t)
             w1_prepare(a)
             if a < 2:
                 load_w1(a + 1)
@@ -239,13 +252,22 @@ def tile_list_contrast_metric_distance_kernel(
                 clear_planes(2)
                 move_scale_rows(2)
             if a == 2:
-                wm_raw = tile([P, PACK, N], F32, "wm_raw")
-                nc.sync.dma_start(wm_raw[:], wm.rearrange("(p t) n -> p t n", t=PACK))
+                wm_rows = wm.rearrange("(p t) n -> p t n", t=PACK)
+                wm_raw = [tile([P, 2, N], F32, "wm_raw%d" % e) for e in range(2)]
+                for e in range(2):
+                    nc.sync.dma_start(wm_raw[e][:], wm_rows[:, 2 * e : 2 * e + 2, :])
             passes(pass_w1, a, (0, 1))
+            if a == 0:
+                passes(pass_w4, a, (0, 1))
+            if a == 1:
+                for t in range(2):
+                    pass_w4(a, 1, t)
             if a == 2:
                 for t in range(2, 4):
-                    pass_w4(a, 0, t)
-            passes(pass_w4, a, (0, 1) if a == 0 else (1,))
+                    pass_w4(1, 1, t)
+                for h in range(HALVES):
+                    for t in range(2, 4):
+                        pass_w4(a, h, t)
 
         gather(LAST)
         for t in range(3):
@@ -257,14 +279,17 @@ def tile_list_contrast_metric_distance_kernel(
             pass_w1(LAST, h, t)
             pass_w4(LAST, h, t, stop=True)
 
+        rows = [tile([P, PACK, HALF], BF16, "rows%d" % h) for h in range(HALVES)]
+
         wm_bf = [tile([P, PACK * N // 2], BF16, "wm_bf%d" % g) for g in range(2)]
         wm_codes = [tile([P, N // 2], U32, "wm_codes%d" % g) for g in range(2)]
         wm_plane = [tile([P, N // 2], U8, "wm_plane%d" % g) for g in range(2)]
-        for g in range(2):
-            nc.vector.tensor_copy(
-                wm_bf[g][:].rearrange("p (m j t) -> p m t j", j=4, t=PACK),
-                wm_raw[:, :, g * (N // 2) : (g + 1) * (N // 2)].rearrange("p t (m j) -> p m t j", j=4),
-            )
+        for e in range(2):
+            for g in range(2):
+                nc.vector.tensor_copy(
+                    wm_bf[g][:].rearrange("p (m j t) -> p m t j", j=4, t=PACK)[:, :, 2 * e : 2 * e + 2, :],
+                    wm_raw[e][:, :, g * (N // 2) : (g + 1) * (N // 2)].rearrange("p t (m j) -> p m t j", j=4),
+                )
 
         def wm_quantise(g):
             nc.vector.quantize_mx(out=wm_codes[g][:].bitcast(FP8X4), scales=wm_plane[g][:], in_=wm_bf[g][:])
@@ -276,7 +301,6 @@ def tile_list_contrast_metric_distance_kernel(
                 rows[:, t, cols], banks[h][t][:, cols], ACT.Square, bias=bias[:, t : t + 1], scale=root[:, t : t + 1]
             )
 
-        rows = [tile([P, PACK, HALF], BF16, "rows%d" % h) for h in range(HALVES)]
         h_rows = [rows[j // 2][:, :, (j % 2) * PART : (j % 2 + 1) * PART] for j in range(PARTS)]
         h_codes = [tile([P, PART], U32, "h_codes%d" % j) for j in range(PARTS)]
         h_plane = [tile([P, PART], U8, "h_plane%d" % j) for j in range(PARTS)]
@@ -320,28 +344,30 @@ def tile_list_contrast_metric_distance_kernel(
                 nc.scalar.activation(dist[:], acc[:], ACT.Sqrt)
                 nc.sync.dma_start(out_rows[:, 2 * pair : 2 * pair + 2, j * PART : (j + 1) * PART], dist[:])
 
-        square_whole(0)
-        square_part(0)
-        square_part(1)
+        square(rows[0], 0, 0, slice(0, HALF))
+        square(rows[0], 0, 1, slice(0, HALF))
+        square(rows[0], 0, 2, slice(0, HALF))
+        square(rows[0], 0, 3, slice(0, PART))
+        square(rows[0], 0, 3, slice(PART, HALF))
         square_whole(1)
         square_part(2)
+        square_part(3)
         h_copy(0)
         wm_quantise(1)
         h_quantise(0)
-        finish_part(0, ("bank00", "bank01"))
-        square_part(3)
         h_copy(1)
         h_copy(2)
         h_quantise(1)
-        h_quantise(2)
-        accs = [psum.tile([P, HALF], F32, name=name) for name in ("bank02", "bank03", "bank10", "bank11")]
-        for j in (1, 2):
-            for u in range(4):
-                metric_product(accs[u][:, (j - 1) * PART : j * PART], u, j)
-        for u in range(4):
-            dist = tile([P, HALF], F32, "dist_mid%d" % u)
-            nc.scalar.activation(dist[:], accs[u][:], ACT.Sqrt)
-            nc.sync.dma_start(out_rows[:, u, PART : 3 * PART], dist[:])
         h_copy(3)
+        h_quantise(2)
         h_quantise(3)
-        finish_part(3, ("bank12", "bank13"))
+        finish_part(0, ("bank00", "bank01"))
+        finish_part(1, ("bank02", "bank03"))
+        accs = [psum.tile([P, HALF], F32, name="bank1%d" % u) for u in range(4)]
+        for j in (2, 3):
+            for u in range(4):
+                metric_product(accs[u][:, (j - 2) * PART : (j - 1) * PART], u, j)
+        for u in range(4):
+            dist = tile([P, HALF], F32, "dist_last%d" % u)
+            nc.scalar.activation(dist[:], accs[u][:], ACT.Sqrt)
+            nc.sync.dma_start(out_rows[:, u, HALF:S], dist[:])

@@ -64,8 +64,8 @@ def tile_list_contrast_metric_distance_kernel(
 
         def tile(shape, dtype, name):
             if name in PLACES:
-                return reuse.tile(shape, dtype, name=name, align_bytes=64, offset=512 * PLACES[name])
-            return keep.tile(shape, dtype, name=name, align_bytes=64)
+                return reuse.tile(shape, dtype, name=name, align_bytes=256, offset=512 * PLACES[name])
+            return keep.tile(shape, dtype, name=name, align_bytes=256)
 
         tab = {}
         w1_raw = {}

@@ -363,11 +363,5 @@ def tile_list_contrast_metric_distance_kernel(
         h_quantise(3)
         finish_part(0, ("bank00", "bank01"))
         finish_part(1, ("bank02", "bank03"))
-        accs = [psum.tile([P, HALF], F32, name="bank1%d" % u) for u in range(4)]
-        for j in (2, 3):
-            for u in range(4):
-                metric_product(accs[u][:, (j - 2) * PART : (j - 1) * PART], u, j)
-        for u in range(4):
-            dist = tile([P, HALF], F32, "dist_last%d" % u)
-            nc.scalar.activation(dist[:], accs[u][:], ACT.Sqrt)
-            nc.sync.dma_start(out_rows[:, u, HALF:S], dist[:])
+        finish_part(2, ("bank10", "bank11"))
+        finish_part(3, ("bank12", "bank13"))

@@ -253,9 +253,9 @@ def tile_list_contrast_metric_distance_kernel(
                 move_scale_rows(2)
             if a == 2:
                 wm_rows = wm.rearrange("(p t) n -> p t n", t=PACK)
-                wm_raw = [tile([P, 2, N], F32, "wm_raw%d" % e) for e in range(2)]
-                for e in range(2):
-                    nc.sync.dma_start(wm_raw[e][:], wm_rows[:, 2 * e : 2 * e + 2, :])
+                wm_raw = [tile([P, PACK, N // 2], F32, "wm_raw%d" % g) for g in range(2)]
+                for g in range(2):
+                    nc.sync.dma_start(wm_raw[g][:], wm_rows[:, :, g * (N // 2) : (g + 1) * (N // 2)])
             passes(pass_w1, a, (0, 1))
             if a == 0:
                 passes(pass_w4, a, (0, 1))
@@ -284,12 +284,11 @@ def tile_list_contrast_metric_distance_kernel(
         wm_bf = [tile([P, PACK * N // 2], BF16, "wm_bf%d" % g) for g in range(2)]
         wm_codes = [tile([P, N // 2], U32, "wm_codes%d" % g) for g in range(2)]
         wm_plane = [tile([P, N // 2], U8, "wm_plane%d" % g) for g in range(2)]
-        for e in range(2):
-            for g in range(2):
-                nc.vector.tensor_copy(
-                    wm_bf[g][:].rearrange("p (m j t) -> p m t j", j=4, t=PACK)[:, :, 2 * e : 2 * e + 2, :],
-                    wm_raw[e][:, :, g * (N // 2) : (g + 1) * (N // 2)].rearrange("p t (m j) -> p m t j", j=4),
-                )
+        for g in range(2):
+            nc.vector.tensor_copy(
+                wm_bf[g][:].rearrange("p (m j t) -> p m t j", j=4, t=PACK),
+                wm_raw[g][:].rearrange("p t (m j) -> p m t j", j=4),
+            )
 
         def wm_quantise(g):
             nc.vector.quantize_mx(out=wm_codes[g][:].bitcast(FP8X4), scales=wm_plane[g][:], in_=wm_bf[g][:])

@@ -49,7 +49,8 @@ PLACES = {
     "tab1": 136,
     "wm_bf0": 168,
     "wm_bf1": 172,
-    "h_bf1": 172,
+    "rows0": 176,
+    "wm_plane1": 176,
 }
 
 
@@ -83,8 +84,8 @@ def tile_list_contrast_metric_distance_kernel(
         def load_w1_last():
             rows = w1[512 * LAST : 512 * (LAST + 1), :].rearrange("(p i) r -> p i r", i=PACK)
             for e in range(2):
-                w1_last[e] = tile([P, 2, H], F32, "w1_last%d" % e)
-                nc.sync.dma_start(w1_last[e][:], rows[:, 2 * e : 2 * e + 2, :])
+                w1_last[e] = tile([P, PACK, H // 2], F32, "w1_last%d" % e)
+                nc.sync.dma_start(w1_last[e][:], rows[:, :, e * (H // 2) : (e + 1) * (H // 2)])
 
         offsets = keep.tile([P, S // 16], U16, name="offsets")
         nc.sync.dma_start(offsets[:], offs)
@@ -137,16 +138,16 @@ def tile_list_contrast_metric_distance_kernel(
                 )
 
         def w1_last_views(e, g):
-            dst = w1_bf[LAST][g][:].rearrange("p (t m i) -> p m t i", t=2, i=PACK)[:, :, :, 2 * e : 2 * e + 2]
+            dst = w1_bf[LAST][g][:].rearrange("p (t m i) -> p m t i", t=2, i=PACK)[:, 64 * e : 64 * e + 64]
             src = w1_last[e][:].rearrange("p i (m t) -> p m t i", t=4)[:, :, 2 * g : 2 * g + 2, :]
             return dst, src
 
-        def w1_last_quantise(t):
-            g, col0 = t // 2, P * (t % 2)
+        def w1_last_quantise(t, first=0, width=P):
+            g, col0 = t // 2, P * (t % 2) + first
             nc.vector.quantize_mx(
-                out=w1_codes[LAST][g][:, col0 : col0 + P].bitcast(FP8X4),
-                scales=w1_plane[LAST][g][:, col0 : col0 + P],
-                in_=w1_bf[LAST][g][:, PACK * col0 : PACK * (col0 + P)],
+                out=w1_codes[LAST][g][:, col0 : col0 + width].bitcast(FP8X4),
+                scales=w1_plane[LAST][g][:, col0 : col0 + width],
+                in_=w1_bf[LAST][g][:, PACK * col0 : PACK * (col0 + width)],
             )
 
         def w1_prepare_last():
@@ -156,10 +157,10 @@ def tile_list_contrast_metric_distance_kernel(
             dst, src = w1_last_views(1, 0)
             nc.vector.tensor_scalar(dst, src, -1.0, None, ALU.mult)
             dst, src = w1_last_views(1, 1)
-            for t in range(2):
-                columns = slice(t * P // 2, (t + 1) * P // 2)
-                nc.vector.tensor_scalar(dst[:, columns], src[:, columns], -1.0, None, ALU.mult)
-                w1_last_quantise(t)
+            nc.scalar.activation(dst, src, ACT.Copy, scale=-1.0)
+            for e in range(2):
+                for t in range(2):
+                    w1_last_quantise(t, e * P // 2, P // 2)
             for t in range(2, 4):
                 w1_last_quantise(t)
 
@@ -270,14 +271,14 @@ def tile_list_contrast_metric_distance_kernel(
                         pass_w4(a, h, t)
 
         gather(LAST)
-        for t in range(3):
+        for t in range(2):
             pass_w4(LAST, 0, t)
         w1_prepare_last()
-        for t in range(3):
+        for t in range(2):
             pass_w1(LAST, 0, t, stop=True)
-        for h, t in [(0, 3)] + [(1, t) for t in range(4)]:
-            pass_w1(LAST, h, t)
-            pass_w4(LAST, h, t, stop=True)
+        for h, t in [(0, 2), (0, 3)] + [(1, t) for t in range(4)]:
+            pass_w4(LAST, h, t)
+            pass_w1(LAST, h, t, stop=True)
 
         rows = [tile([P, PACK, HALF], BF16, "rows%d" % h) for h in range(HALVES)]
 
@@ -348,15 +349,16 @@ def tile_list_contrast_metric_distance_kernel(
         square(rows[0], 0, 2, slice(0, HALF))
         square(rows[0], 0, 3, slice(0, PART))
         square(rows[0], 0, 3, slice(PART, HALF))
-        square_whole(1)
-        square_part(2)
-        square_part(3)
+        for t in range(3):
+            square(rows[1], 1, t, slice(0, HALF))
+        square(rows[1], 1, 3, slice(0, PART))
+        square(rows[1], 1, 3, slice(PART, HALF))
         h_copy(0)
-        wm_quantise(1)
-        h_quantise(0)
         h_copy(1)
-        h_copy(2)
+        h_quantise(0)
+        wm_quantise(1)
         h_quantise(1)
+        h_copy(2)
         h_copy(3)
         h_quantise(2)
         h_quantise(3)

@@ -18,38 +18,46 @@ ALU = mybir.AluOpType
 
 P = 128
 PACK = 4
-PASSES = K // (P * PACK)
+K_PASS = P * PACK
+PASSES = K // K_PASS
+LAST = PASSES - 1
+TILES = H // P
+PAIRS = TILES // 2
+BLOCKS = 16
 HALF = 512
 HALVES = S // HALF
 PART = 256
 PARTS = S // PART
 ROW0 = 32
 ROW_BYTES = S + H
-SHARED_FROM = 1
-LAST = PASSES - 1
+SHARED_PASS = 1
+LATE_PASS = LAST - 1
+AHEAD = 2
+
+PLACE_BYTES = 512
 PLACES = {
+    "picked_scales": 135,
+    "w4_raw": 128,
+    "tab1": 136,
+    "tab0": 96,
+    "gain_sb": 96,
+    "c_sb": 97,
+    "planes1": 98,
     "w1_raw0": 48,
     "w1_raw1": 34,
     "planes2": 60,
     "tab2": 63,
     "w1_raw2": 44,
-    "planes3": 80,
     "tab3": 4,
     "w1_last0": 64,
     "w1_last1": 72,
+    "planes3": 80,
     "wm_raw0": 44,
     "wm_raw1": 52,
     "w1_bf31": 170,
-    "tab0": 96,
-    "gain_sb": 96,
-    "c_sb": 97,
-    "planes1": 98,
-    "w4_raw": 128,
-    "picked_scales": 135,
-    "tab1": 136,
     "wm_bf0": 168,
     "wm_bf1": 172,
-    "rows0": 176,
+    "squares0": 176,
     "wm_plane1": 176,
 }
 
@@ -65,38 +73,42 @@ def tile_list_contrast_metric_distance_kernel(
 
         def tile(shape, dtype, name):
             if name in PLACES:
-                return reuse.tile(shape, dtype, name=name, align_bytes=256, offset=512 * PLACES[name])
+                return reuse.tile(shape, dtype, name=name, align_bytes=256, offset=PLACE_BYTES * PLACES[name])
             return keep.tile(shape, dtype, name=name, align_bytes=256)
 
         tab = {}
         w1_raw = {}
+        w1_last = {}
 
         def load_tab(a):
             tab[a] = tile([P, T], I32, "tab%d" % a)
             nc.sync.dma_start(tab[a][:], tab_words[a].rearrange("p t i -> p (t i)").bitcast(I32))
 
+        def w1_rows(a):
+            return w1[K_PASS * a : K_PASS * (a + 1), :].rearrange("(p i) r -> p i r", i=PACK)
+
         def load_w1(a):
             w1_raw[a] = tile([P, PACK, H], F32, "w1_raw%d" % a)
-            nc.sync.dma_start(w1_raw[a][:], w1[512 * a : 512 * (a + 1), :].rearrange("(p i) r -> p i r", i=PACK))
-
-        w1_last = {}
+            nc.sync.dma_start(w1_raw[a][:], w1_rows(a))
 
         def load_w1_last():
-            rows = w1[512 * LAST : 512 * (LAST + 1), :].rearrange("(p i) r -> p i r", i=PACK)
+            rows = w1_rows(LAST)
             for e in range(2):
                 w1_last[e] = tile([P, PACK, H // 2], F32, "w1_last%d" % e)
                 nc.sync.dma_start(w1_last[e][:], rows[:, :, e * (H // 2) : (e + 1) * (H // 2)])
 
         offsets = keep.tile([P, S // 16], U16, name="offsets")
-        nc.sync.dma_start(offsets[:], offs)
         tab_scale_rows = tile([P, T // 4], I32, "tab_scale_rows")
         w4_scale_rows = tile([P, H // 4], I32, "w4_scale_rows")
-        for rows, scales in ((tab_scale_rows, tab_scales), (w4_scale_rows, w4_scales)):
-            nc.vector.memset(rows[0:ROW0, :], 0)
-            nc.vector.memset(rows[ROW0 + 64 : P, :], 0)
-            nc.sync.dma_start(rows[ROW0 : ROW0 + 64, :], scales.rearrange("a q e -> (a q) e").bitcast(I32))
+        row_end = ROW0 + PASSES * BLOCKS
+        for raw_rows, scales in ((tab_scale_rows, tab_scales), (w4_scale_rows, w4_scales)):
+            nc.vector.memset(raw_rows[0:ROW0, :], 0)
+            nc.vector.memset(raw_rows[row_end:P, :], 0)
+            nc.sync.dma_start(raw_rows[ROW0:row_end, :], scales.rearrange("a q e -> (a q) e").bitcast(I32))
+        nc.sync.dma_start(offsets[:], offs)
         load_tab(0)
         load_w1(0)
+
         planes = {}
 
         def clear_planes(a):
@@ -104,45 +116,51 @@ def tile_list_contrast_metric_distance_kernel(
             nc.vector.memset(planes[a][:], 0)
 
         def move_scale_rows(a):
-            first = ROW0 + 16 * a
+            first = ROW0 + BLOCKS * a
             for r in range(4):
-                nc.sync.dma_start(planes[a][r:P:32, :], scale_rows[first + r : first + 16 : 4, :])
+                nc.sync.dma_start(planes[a][r:P:32, :], scale_rows[first + r : first + BLOCKS : 4, :])
+
+        def plane(a, first, width):
+            return planes[a][:].bitcast(U8)[:, first : first + width]
 
         clear_planes(0)
 
-        banks = [[psum.tile([P, HALF], F32, name="bank%d%d" % (h, t)) for t in range(4)] for h in range(HALVES)]
+        banks = [[psum.tile([P, HALF], F32, name="bank%d%d" % (h, t)) for t in range(TILES)] for h in range(HALVES)]
         picked = [[] for a in range(PASSES)]
-        w1_bf = [[tile([P, PACK * H // 2], BF16, "w1_bf%d%d" % (a, g)) for g in range(2)] for a in range(PASSES)]
-        w1_codes = [[tile([P, H // 2], U32, "w1_codes%d%d" % (a, g)) for g in range(2)] for a in range(PASSES)]
-        w1_plane = [[tile([P, H // 2], U8, "w1_plane%d%d" % (a, g)) for g in range(2)] for a in range(PASSES)]
+        w1_bf = [[tile([P, PACK * H // 2], BF16, "w1_bf%d%d" % (a, g)) for g in range(PAIRS)] for a in range(PASSES)]
+        w1_codes = [[tile([P, H // 2], U32, "w1_codes%d%d" % (a, g)) for g in range(PAIRS)] for a in range(PASSES)]
+        w1_plane = [[tile([P, H // 2], U8, "w1_plane%d%d" % (a, g)) for g in range(PAIRS)] for a in range(PASSES)]
 
         def gather(a):
             for h in range(HALVES):
                 picked[a].append(tile([P, HALF], U32, "picked%d%d" % (a, h)))
-                cols = offsets[:, h * (HALF // 16) : (h + 1) * (HALF // 16)]
-                nc.vector.tensor_copy(picked[a][h][:], tab[a][:].bitcast(U32).indirect(cols))
+                entries = offsets[:, h * (HALF // 16) : (h + 1) * (HALF // 16)]
+                nc.vector.tensor_copy(picked[a][h][:], tab[a][:].bitcast(U32).indirect(entries))
+
+        def word_view(a, g):
+            return w1_bf[a][g][:].rearrange("p (t m i) -> p m t i", t=2, i=PACK)
+
+        def pair_view(raw, g):
+            return raw[:].rearrange("p i (m t) -> p m t i", t=TILES)[:, :, 2 * g : 2 * g + 2, :]
+
+        def round_on_vector(dst, src):
+            nc.vector.tensor_scalar(dst, src, -1.0, None, ALU.mult)
+
+        def round_on_scalar(dst, src):
+            nc.scalar.activation(dst, src, ACT.Copy, scale=-1.0)
 
         def w1_prepare(a):
-            for g in range(2):
-                dst = w1_bf[a][g][:].rearrange("p (t m i) -> p m t i", t=2, i=PACK)
-                src = w1_raw[a][:].rearrange("p i (m t) -> p m t i", t=4)[:, :, 2 * g : 2 * g + 2, :]
-                if a == SHARED_FROM and g == 0:
-                    nc.vector.tensor_scalar(dst, src, -1.0, None, ALU.mult)
-                else:
-                    nc.scalar.activation(dst, src, ACT.Copy, scale=-1.0)
-            for g in range(2):
+            for g in range(PAIRS):
+                round_w1 = round_on_vector if (a, g) == (SHARED_PASS, 0) else round_on_scalar
+                round_w1(word_view(a, g), pair_view(w1_raw[a], g))
+            for g in range(PAIRS):
                 nc.vector.quantize_mx(
                     out=w1_codes[a][g][:].bitcast(FP8X4),
                     scales=w1_plane[a][g][:],
                     in_=w1_bf[a][g][:],
                 )
 
-        def w1_last_views(e, g):
-            dst = w1_bf[LAST][g][:].rearrange("p (t m i) -> p m t i", t=2, i=PACK)[:, 64 * e : 64 * e + 64]
-            src = w1_last[e][:].rearrange("p i (m t) -> p m t i", t=4)[:, :, 2 * g : 2 * g + 2, :]
-            return dst, src
-
-        def w1_last_quantise(t, first=0, width=P):
+        def w1_last_quantise(t, first, width):
             g, col0 = t // 2, P * (t % 2) + first
             nc.vector.quantize_mx(
                 out=w1_codes[LAST][g][:, col0 : col0 + width].bitcast(FP8X4),
@@ -151,23 +169,18 @@ def tile_list_contrast_metric_distance_kernel(
             )
 
         def w1_prepare_last():
-            for g in range(2):
-                dst, src = w1_last_views(0, g)
-                nc.scalar.activation(dst, src, ACT.Copy, scale=-1.0)
-            dst, src = w1_last_views(1, 0)
-            nc.vector.tensor_scalar(dst, src, -1.0, None, ALU.mult)
-            dst, src = w1_last_views(1, 1)
-            nc.scalar.activation(dst, src, ACT.Copy, scale=-1.0)
+            half = P // 2
+            for e in range(2):
+                for g in range(PAIRS):
+                    round_w1 = round_on_vector if (e, g) == (1, 0) else round_on_scalar
+                    round_w1(word_view(LAST, g)[:, half * e : half * (e + 1)], pair_view(w1_last[e], g))
             for e in range(2):
                 for t in range(2):
-                    w1_last_quantise(t, e * P // 2, P // 2)
-            for t in range(2, 4):
-                w1_last_quantise(t)
+                    w1_last_quantise(t, e * half, half)
+            for t in range(2, TILES):
+                w1_last_quantise(t, 0, P)
 
-        def plane(a, first, width):
-            return planes[a][:].bitcast(U8)[:, first : first + width]
-
-        def pass_w4(a, h, t, stop=False):
+        def pass_w4(a, h, t):
             col0 = (t * PASSES + a) * P
             nc.tensor.matmul_mx(
                 out=banks[h][t][:],
@@ -176,10 +189,10 @@ def tile_list_contrast_metric_distance_kernel(
                 rhs=picked[a][h][:].bitcast(FP8X4),
                 rhs_scale=plane(a, h * HALF, HALF),
                 start=False,
-                stop=stop,
+                stop=False,
             )
 
-        def pass_w1(a, h, t, stop=False):
+        def pass_w1(a, h, t):
             nc.tensor.matmul_mx(
                 out=banks[h][t][:],
                 lhsT=w1_codes[a][t // 2][:, P * (t % 2) : P * (t % 2 + 1)].bitcast(FP8X4),
@@ -187,20 +200,25 @@ def tile_list_contrast_metric_distance_kernel(
                 rhs=picked[a][h][:].bitcast(FP8X4),
                 rhs_scale=plane(a, h * HALF, HALF),
                 start=(a == 0),
-                stop=stop,
+                stop=(a == LAST),
             )
 
-        def passes(one_pass, a, halves):
+        def passes(one_pass, a, halves, tiles):
             for h in halves:
-                for t in range(4):
+                for t in tiles:
                     one_pass(a, h, t)
+
+        both_halves = range(HALVES)
+        all_tiles = range(TILES)
+        first_pair = range(0, 2)
+        second_pair = range(2, TILES)
 
         scale_rows = tile([P, ROW_BYTES // 4], I32, "scale_rows")
         picked_scales = tile([P, S], U8, "picked_scales")
         nc.vector.tensor_copy(picked_scales[:], tab_scale_rows[:].bitcast(U8).indirect(offsets[:]))
         nc.vector.tensor_copy(
-            scale_rows[:].bitcast(U8)[:, S:ROW_BYTES].rearrange("p (t m) -> p t m", t=4),
-            w4_scale_rows[:].bitcast(U8).rearrange("p (m t) -> p t m", t=4),
+            scale_rows[:].bitcast(U8)[:, S:ROW_BYTES].rearrange("p (t m) -> p t m", t=TILES),
+            w4_scale_rows[:].bitcast(U8).rearrange("p (m t) -> p t m", t=TILES),
         )
         nc.vector.tensor_copy(scale_rows[:, 0 : S // 4], picked_scales[:].bitcast(I32))
         move_scale_rows(0)
@@ -211,81 +229,75 @@ def tile_list_contrast_metric_distance_kernel(
         load_tab(1)
 
         gather(0)
-        gain_sb = tile([P, 4], F32, "gain_sb")
-        nc.sync.dma_start(gain_sb[:], gain.rearrange("(p t) -> p t", t=4))
-        c_sb = tile([P, 4], F32, "c_sb")
-        nc.sync.dma_start(c_sb[:], c.rearrange("(p t) -> p t", t=4))
+        gain_sb = tile([P, TILES], F32, "gain_sb")
+        nc.sync.dma_start(gain_sb[:], gain.rearrange("(p t) -> p t", t=TILES))
+        c_sb = tile([P, TILES], F32, "c_sb")
+        nc.sync.dma_start(c_sb[:], c.rearrange("(p t) -> p t", t=TILES))
         clear_planes(1)
         move_scale_rows(1)
-        root0 = tile([P, 4], F32, "root0")
-        inv = tile([P, 4], F32, "inv")
-        quot = tile([P, 4], F32, "quot")
-        both = tile([P, 4], F32, "both")
-        root = tile([P, 4], F32, "root")
-        bias = tile([P, 4], F32, "bias")
-        nc.scalar.activation(root0[:], gain_sb[:], ACT.Sqrt)
-        nc.vector.reciprocal(inv[:], root0[:])
+        guess = tile([P, TILES], F32, "guess")
+        inv = tile([P, TILES], F32, "inv")
+        quot = tile([P, TILES], F32, "quot")
+        twice = tile([P, TILES], F32, "twice")
+        root = tile([P, TILES], F32, "root")
+        bias = tile([P, TILES], F32, "bias")
+        nc.scalar.activation(guess[:], gain_sb[:], ACT.Sqrt)
+        nc.vector.reciprocal(inv[:], guess[:])
         nc.vector.tensor_tensor(quot[:], gain_sb[:], inv[:], ALU.mult)
-        nc.vector.tensor_tensor(both[:], quot[:], root0[:], ALU.add)
-        nc.vector.tensor_scalar(root[:], both[:], 0.5, None, ALU.mult)
+        nc.vector.tensor_tensor(twice[:], quot[:], guess[:], ALU.add)
+        nc.vector.tensor_scalar(root[:], twice[:], 0.5, None, ALU.mult)
         nc.vector.tensor_tensor(bias[:], root[:], c_sb[:], ALU.mult)
 
         w4_codes = tile([P, PASSES * H // 2], I32, "w4_codes")
         nc.vector.tensor_copy(
-            w4_codes[:].bitcast(U16).rearrange("p (t m) -> p t m", t=4),
-            w4_raw[:].bitcast(U16).rearrange("p (m t) -> p t m", t=4),
+            w4_codes[:].bitcast(U16).rearrange("p (t m) -> p t m", t=TILES),
+            w4_raw[:].bitcast(U16).rearrange("p (m t) -> p t m", t=TILES),
         )
 
         for a in range(LAST):
             if a > 0:
                 gather(a)
-                if a == 2:
-                    load_w1_last()
-                    clear_planes(LAST)
-                    move_scale_rows(LAST)
-                for h, t in [(0, t) for t in range(4)] if a < 2 else [(0, 0), (0, 1), (1, 0), (1, 1)]:
-                    pass_w4(a, h, t)
+            if a == LATE_PASS:
+                load_w1_last()
+                clear_planes(LAST)
+                move_scale_rows(LAST)
+                passes(pass_w4, a, both_halves, first_pair)
             w1_prepare(a)
-            if a < 2:
+            if a < LATE_PASS:
                 load_w1(a + 1)
                 load_tab(a + 2)
             if a == 0:
-                clear_planes(2)
-                move_scale_rows(2)
-            if a == 2:
+                clear_planes(LATE_PASS)
+                move_scale_rows(LATE_PASS)
+            if a == LATE_PASS:
                 wm_rows = wm.rearrange("(p t) n -> p t n", t=PACK)
-                wm_raw = [tile([P, PACK, N // 2], F32, "wm_raw%d" % g) for g in range(2)]
-                for g in range(2):
+                wm_raw = [tile([P, PACK, N // 2], F32, "wm_raw%d" % g) for g in range(PAIRS)]
+                for g in range(PAIRS):
                     nc.sync.dma_start(wm_raw[g][:], wm_rows[:, :, g * (N // 2) : (g + 1) * (N // 2)])
-            passes(pass_w1, a, (0, 1))
+            passes(pass_w1, a, both_halves, all_tiles)
             if a == 0:
-                passes(pass_w4, a, (0, 1))
-            if a == 1:
-                for t in range(2):
-                    pass_w4(a, 1, t)
-            if a == 2:
-                for t in range(2, 4):
-                    pass_w4(1, 1, t)
-                for h in range(HALVES):
-                    for t in range(2, 4):
-                        pass_w4(a, h, t)
+                passes(pass_w4, a, both_halves, all_tiles)
+            elif a < LATE_PASS:
+                passes(pass_w4, a, (0,), all_tiles)
+                passes(pass_w4, a, (1,), first_pair)
+            else:
+                passes(pass_w4, a - 1, (1,), second_pair)
+                passes(pass_w4, a, both_halves, second_pair)
 
         gather(LAST)
-        for t in range(2):
-            pass_w4(LAST, 0, t)
+        passes(pass_w4, LAST, (0,), range(AHEAD))
         w1_prepare_last()
-        for t in range(2):
-            pass_w1(LAST, 0, t, stop=True)
-        for h, t in [(0, 2), (0, 3)] + [(1, t) for t in range(4)]:
-            pass_w4(LAST, h, t)
-            pass_w1(LAST, h, t, stop=True)
+        for h in both_halves:
+            for t in all_tiles:
+                if h > 0 or t >= AHEAD:
+                    pass_w4(LAST, h, t)
+                pass_w1(LAST, h, t)
 
-        rows = [tile([P, PACK, HALF], BF16, "rows%d" % h) for h in range(HALVES)]
-
-        wm_bf = [tile([P, PACK * N // 2], BF16, "wm_bf%d" % g) for g in range(2)]
-        wm_codes = [tile([P, N // 2], U32, "wm_codes%d" % g) for g in range(2)]
-        wm_plane = [tile([P, N // 2], U8, "wm_plane%d" % g) for g in range(2)]
-        for g in range(2):
+        squares = [tile([P, TILES, HALF], BF16, "squares%d" % h) for h in both_halves]
+        wm_bf = [tile([P, PACK * N // 2], BF16, "wm_bf%d" % g) for g in range(PAIRS)]
+        wm_codes = [tile([P, N // 2], U32, "wm_codes%d" % g) for g in range(PAIRS)]
+        wm_plane = [tile([P, N // 2], U8, "wm_plane%d" % g) for g in range(PAIRS)]
+        for g in range(PAIRS):
             nc.vector.tensor_copy(
                 wm_bf[g][:].rearrange("p (m j t) -> p m t j", j=4, t=PACK),
                 wm_raw[g][:].rearrange("p t (m j) -> p m t j", j=4),
@@ -296,63 +308,51 @@ def tile_list_contrast_metric_distance_kernel(
 
         wm_quantise(0)
 
-        def square(rows, h, t, cols):
-            nc.scalar.activation(
-                rows[:, t, cols], banks[h][t][:, cols], ACT.Square, bias=bias[:, t : t + 1], scale=root[:, t : t + 1]
-            )
-
-        h_rows = [rows[j // 2][:, :, (j % 2) * PART : (j % 2 + 1) * PART] for j in range(PARTS)]
         h_codes = [tile([P, PART], U32, "h_codes%d" % j) for j in range(PARTS)]
         h_plane = [tile([P, PART], U8, "h_plane%d" % j) for j in range(PARTS)]
         h_bf = [tile([P, PACK * PART], BF16, "h_bf%d" % j) for j in range(PARTS)]
         out_rows = out.rearrange("(u p) j -> p u j", p=P)
 
-        def square_whole(h):
-            for t in range(2):
-                square(rows[h], h, t, slice(0, HALF))
-
-        def square_part(j):
-            for t in range(2, 4):
-                square(rows[j // 2], j // 2, t, slice((j % 2) * PART, (j % 2 + 1) * PART))
+        def square(h, t, cols):
+            nc.scalar.activation(
+                squares[h][:, t, cols],
+                banks[h][t][:, cols],
+                ACT.Square,
+                bias=bias[:, t : t + 1],
+                scale=root[:, t : t + 1],
+            )
 
         def h_copy(j):
             nc.vector.tensor_copy(
                 h_bf[j][:].rearrange("p (m i t) -> p m t i", i=4, t=PACK),
-                h_rows[j].rearrange("p t (m i) -> p m t i", i=4),
+                squares[j // 2][:, :, (j % 2) * PART : (j % 2 + 1) * PART].rearrange("p t (m i) -> p m t i", i=4),
             )
 
         def h_quantise(j):
             nc.vector.quantize_mx(out=h_codes[j][:].bitcast(FP8X4), scales=h_plane[j][:], in_=h_bf[j][:])
 
-        def metric_product(acc, u, j):
-            nc.tensor.matmul_mx(
-                out=acc,
-                lhsT=wm_codes[u // 2][:, P * (u % 2) : P * (u % 2 + 1)].bitcast(FP8X4),
-                lhsT_scale=wm_plane[u // 2][:, P * (u % 2) : P * (u % 2 + 1)],
-                rhs=h_codes[j][:].bitcast(FP8X4),
-                rhs_scale=h_plane[j][:],
-                start=True,
-                stop=True,
-            )
-
-        def finish_part(j, names):
-            for pair in range(2):
-                acc = psum.tile([P, 2, PART], F32, name=names[pair])
+        def finish_part(j):
+            for g in range(PAIRS):
+                acc = psum.tile([P, 2, PART], F32, name="bank%d%d" % (j // 2, 2 * (j % 2) + g))
                 for e in range(2):
-                    metric_product(acc[:, e, :], 2 * pair + e, j)
-                dist = tile([P, 2, PART], F32, "dist%d%d" % (j, pair))
+                    nc.tensor.matmul_mx(
+                        out=acc[:, e, :],
+                        lhsT=wm_codes[g][:, P * e : P * (e + 1)].bitcast(FP8X4),
+                        lhsT_scale=wm_plane[g][:, P * e : P * (e + 1)],
+                        rhs=h_codes[j][:].bitcast(FP8X4),
+                        rhs_scale=h_plane[j][:],
+                        start=True,
+                        stop=True,
+                    )
+                dist = tile([P, 2, PART], F32, "dist%d%d" % (j, g))
                 nc.scalar.activation(dist[:], acc[:], ACT.Sqrt)
-                nc.sync.dma_start(out_rows[:, 2 * pair : 2 * pair + 2, j * PART : (j + 1) * PART], dist[:])
+                nc.sync.dma_start(out_rows[:, 2 * g : 2 * g + 2, j * PART : (j + 1) * PART], dist[:])
 
-        square(rows[0], 0, 0, slice(0, HALF))
-        square(rows[0], 0, 1, slice(0, HALF))
-        square(rows[0], 0, 2, slice(0, HALF))
-        square(rows[0], 0, 3, slice(0, PART))
-        square(rows[0], 0, 3, slice(PART, HALF))
-        for t in range(3):
-            square(rows[1], 1, t, slice(0, HALF))
-        square(rows[1], 1, 3, slice(0, PART))
-        square(rows[1], 1, 3, slice(PART, HALF))
+        for h in both_halves:
+            for t in range(TILES - 1):
+                square(h, t, slice(0, HALF))
+            for first in range(0, HALF, PART):
+                square(h, TILES - 1, slice(first, first + PART))
         h_copy(0)
         h_copy(1)
         h_quantise(0)
@@ -362,7 +362,5 @@ def tile_list_contrast_metric_distance_kernel(
         h_copy(3)
         h_quantise(2)
         h_quantise(3)
-        finish_part(0, ("bank00", "bank01"))
-        finish_part(1, ("bank02", "bank03"))
-        finish_part(2, ("bank10", "bank11"))
-        finish_part(3, ("bank12", "bank13"))
+        for j in range(PARTS):
+            finish_part(j)

@@ -55,10 +55,11 @@ PLACES = {
     "wm_raw0": 44,
     "wm_raw1": 52,
     "w1_bf31": 170,
-    "wm_bf0": 168,
-    "wm_bf1": 172,
-    "squares0": 176,
-    "wm_plane1": 176,
+    "wm_bf0": 167,
+    "picked_late": 171,
+    "wm_bf1": 173,
+    "squares0": 177,
+    "wm_plane1": 177,
 }
 
 
@@ -180,28 +181,35 @@ def tile_list_contrast_metric_distance_kernel(
             for t in range(2, TILES):
                 w1_last_quantise(t, 0, P)
 
+        def pieces(a, h):
+            if (a, h) == (LAST, HALVES - 1):
+                return [(picked[a][h], 0, PART), (picked[a][h + 1], PART, PART)]
+            return [(picked[a][h], 0, HALF)]
+
         def pass_w4(a, h, t):
             col0 = (t * PASSES + a) * P
-            nc.tensor.matmul_mx(
-                out=banks[h][t][:],
-                lhsT=w4_codes[:, col0 // 2 : (col0 + P) // 2].bitcast(FP4X4),
-                lhsT_scale=plane(a, S + t * P, P),
-                rhs=picked[a][h][:].bitcast(FP8X4),
-                rhs_scale=plane(a, h * HALF, HALF),
-                start=False,
-                stop=False,
-            )
+            for words, first, width in pieces(a, h):
+                nc.tensor.matmul_mx(
+                    out=banks[h][t][:, first : first + width],
+                    lhsT=w4_codes[:, col0 // 2 : (col0 + P) // 2].bitcast(FP4X4),
+                    lhsT_scale=plane(a, S + t * P, P),
+                    rhs=words[:].bitcast(FP8X4),
+                    rhs_scale=plane(a, h * HALF + first, width),
+                    start=False,
+                    stop=False,
+                )
 
         def pass_w1(a, h, t):
-            nc.tensor.matmul_mx(
-                out=banks[h][t][:],
-                lhsT=w1_codes[a][t // 2][:, P * (t % 2) : P * (t % 2 + 1)].bitcast(FP8X4),
-                lhsT_scale=w1_plane[a][t // 2][:, P * (t % 2) : P * (t % 2 + 1)],
-                rhs=picked[a][h][:].bitcast(FP8X4),
-                rhs_scale=plane(a, h * HALF, HALF),
-                start=(a == 0),
-                stop=(a == LAST),
-            )
+            for words, first, width in pieces(a, h):
+                nc.tensor.matmul_mx(
+                    out=banks[h][t][:, first : first + width],
+                    lhsT=w1_codes[a][t // 2][:, P * (t % 2) : P * (t % 2 + 1)].bitcast(FP8X4),
+                    lhsT_scale=w1_plane[a][t // 2][:, P * (t % 2) : P * (t % 2 + 1)],
+                    rhs=words[:].bitcast(FP8X4),
+                    rhs_scale=plane(a, h * HALF + first, width),
+                    start=(a == 0),
+                    stop=(a == LAST and first + width == HALF),
+                )
 
         def passes(one_pass, a, halves, tiles):
             for h in halves:
@@ -284,9 +292,16 @@ def tile_list_contrast_metric_distance_kernel(
                 passes(pass_w4, a - 1, (1,), second_pair)
                 passes(pass_w4, a, both_halves, second_pair)
 
-        gather(LAST)
+        def gather_last(name, first, width):
+            picked[LAST].append(tile([P, width], U32, name))
+            entries = offsets[:, first // 16 : (first + width) // 16]
+            nc.vector.tensor_copy(picked[LAST][-1][:], tab[LAST][:].bitcast(U32).indirect(entries))
+
+        gather_last("picked30", 0, HALF)
+        gather_last("picked31", HALF, PART)
         passes(pass_w4, LAST, (0,), range(AHEAD))
         w1_prepare_last()
+        gather_last("picked_late", HALF + PART, PART)
         for h in both_halves:
             for t in all_tiles:
                 if h > 0 or t >= AHEAD:
@@ -346,7 +361,8 @@ def tile_list_contrast_metric_distance_kernel(
                     )
                 dist = tile([P, 2, PART], F32, "dist%d%d" % (j, g))
                 nc.scalar.activation(dist[:], acc[:], ACT.Sqrt)
-                nc.sync.dma_start(out_rows[:, 2 * g : 2 * g + 2, j * PART : (j + 1) * PART], dist[:])
+                queue = nc.scalar if (j, g) == (PARTS - 1, PAIRS - 1) else nc.sync
+                queue.dma_start(out_rows[:, 2 * g : 2 * g + 2, j * PART : (j + 1) * PART], dist[:])
 
         for h in both_halves:
             for t in range(TILES - 1):

@@ -32,7 +32,7 @@ ROW0 = 32
 ROW_BYTES = S + H
 SHARED_PASS = 1
 LATE_PASS = LAST - 1
-AHEAD = 2
+AHEAD = 1
 
 PLACE_BYTES = 512
 PLACES = {
@@ -173,8 +173,12 @@ def tile_list_contrast_metric_distance_kernel(
             half = P // 2
             for e in range(2):
                 for g in range(PAIRS):
-                    round_w1 = round_on_vector if (e, g) == (1, 0) else round_on_scalar
-                    round_w1(word_view(LAST, g)[:, half * e : half * (e + 1)], pair_view(w1_last[e], g))
+                    dst, src = word_view(LAST, g)[:, half * e : half * (e + 1)], pair_view(w1_last[e], g)
+                    if (e, g) == (1, 0):
+                        for t in range(2):
+                            round_on_vector(dst[:, :, t, :], src[:, :, t, :])
+                    else:
+                        round_on_scalar(dst, src)
             for e in range(2):
                 for t in range(2):
                     w1_last_quantise(t, e * half, half)

@@ -33,6 +33,7 @@ ROW_BYTES = S + H
 SHARED_PASS = 1
 LATE_PASS = LAST - 1
 AHEAD = 1
+SHARE = 128
 
 PLACE_BYTES = 512
 PLACES = {
@@ -58,8 +59,12 @@ PLACES = {
     "wm_bf0": 167,
     "picked_late": 171,
     "wm_bf1": 173,
-    "squares0": 177,
-    "wm_plane1": 177,
+    "h_bf0": 181,
+    "wm_plane1": 181,
+    "h_bf256": 182,
+    "h_bf512": 189,
+    "h_bf768": 190,
+    "h_bf896": 188,
 }
 
 
@@ -315,7 +320,7 @@ def tile_list_contrast_metric_distance_kernel(
         squares = [tile([P, TILES, HALF], BF16, "squares%d" % h) for h in both_halves]
         wm_bf = [tile([P, PACK * N // 2], BF16, "wm_bf%d" % g) for g in range(PAIRS)]
         wm_codes = [tile([P, N // 2], U32, "wm_codes%d" % g) for g in range(PAIRS)]
-        wm_plane = [tile([P, N // 2], U8, "wm_plane%d" % g) for g in range(PAIRS)]
+        wm_plane = {}
         for g in range(PAIRS):
             nc.vector.tensor_copy(
                 wm_bf[g][:].rearrange("p (m j t) -> p m t j", j=4, t=PACK),
@@ -323,13 +328,14 @@ def tile_list_contrast_metric_distance_kernel(
             )
 
         def wm_quantise(g):
+            wm_plane[g] = tile([P, N // 2], U8, "wm_plane%d" % g)
             nc.vector.quantize_mx(out=wm_codes[g][:].bitcast(FP8X4), scales=wm_plane[g][:], in_=wm_bf[g][:])
 
         wm_quantise(0)
 
         h_codes = [tile([P, PART], U32, "h_codes%d" % j) for j in range(PARTS)]
         h_plane = [tile([P, PART], U8, "h_plane%d" % j) for j in range(PARTS)]
-        h_bf = [tile([P, PACK * PART], BF16, "h_bf%d" % j) for j in range(PARTS)]
+        h_bf = {}
         out_rows = out.rearrange("(u p) j -> p u j", p=P)
 
         def square(h, t, cols):
@@ -341,14 +347,26 @@ def tile_list_contrast_metric_distance_kernel(
                 scale=root[:, t : t + 1],
             )
 
-        def h_copy(j):
+        def h_copy(first, width):
+            h_bf[first] = tile([P, PACK * width], BF16, "h_bf%d" % first)
+            col0 = first % HALF
             nc.vector.tensor_copy(
-                h_bf[j][:].rearrange("p (m i t) -> p m t i", i=4, t=PACK),
-                squares[j // 2][:, :, (j % 2) * PART : (j % 2 + 1) * PART].rearrange("p t (m i) -> p m t i", i=4),
+                h_bf[first][:].rearrange("p (m i t) -> p m t i", i=4, t=PACK),
+                squares[first // HALF][:, :, col0 : col0 + width].rearrange("p t (m i) -> p m t i", i=4),
             )
 
-        def h_quantise(j):
-            nc.vector.quantize_mx(out=h_codes[j][:].bitcast(FP8X4), scales=h_plane[j][:], in_=h_bf[j][:])
+        def h_quantise(first, width):
+            j, col0 = first // PART, first % PART
+            nc.vector.quantize_mx(
+                out=h_codes[j][:, col0 : col0 + width].bitcast(FP8X4),
+                scales=h_plane[j][:, col0 : col0 + width],
+                in_=h_bf[first][:],
+            )
+
+        def h_in_halves(j):
+            for step in (h_copy, h_quantise):
+                for first in range(j * PART, (j + 1) * PART, PART // 2):
+                    step(first, PART // 2)
 
         def finish_part(j):
             for g in range(PAIRS):
@@ -368,19 +386,27 @@ def tile_list_contrast_metric_distance_kernel(
                 queue = nc.scalar if (j, g) == (PARTS - 1, PAIRS - 1) else nc.sync
                 queue.dma_start(out_rows[:, 2 * g : 2 * g + 2, j * PART : (j + 1) * PART], dist[:])
 
-        for h in both_halves:
-            for t in range(TILES - 1):
-                square(h, t, slice(0, HALF))
-            for first in range(0, HALF, PART):
-                square(h, TILES - 1, slice(first, first + PART))
-        h_copy(0)
-        h_copy(1)
-        h_quantise(0)
+        last = TILES - 1
+        for t in range(last):
+            square(0, t, slice(0, HALF))
+        for first in range(0, HALF, PART):
+            square(0, last, slice(first, first + PART))
+        for t in range(last):
+            square(1, t, slice(0, HALF))
+        square(1, last, slice(0, HALF - SHARE))
+        h_in_halves(0)
+        h_copy(PART, PART)
         wm_quantise(1)
-        h_quantise(1)
-        h_copy(2)
-        h_copy(3)
-        h_quantise(2)
-        h_quantise(3)
+        h_quantise(PART, PART)
+        shifted = tile([P, SHARE], F32, "shifted")
+        h_copy(2 * PART, P)
+        nc.vector.tensor_scalar(
+            shifted[:], banks[1][last][:, HALF - SHARE : HALF], root[:, last:TILES], bias[:, last:TILES], ALU.mult, ALU.add
+        )
+        h_copy(2 * PART + P, P)
+        h_quantise(2 * PART, P)
+        h_quantise(2 * PART + P, P)
+        nc.vector.tensor_tensor(squares[1][:, last, HALF - SHARE : HALF], shifted[:], shifted[:], ALU.mult)
+        h_in_halves(3)
         for j in range(PARTS):
             finish_part(j)

from contextlib import ExitStack

import concourse.mybir as mybir

K, H, N, T, S = 2048, 512, 512, 4096, 1024
FLOPS = 2 * (2 * K * H * S + H * N * S)

F32 = mybir.dt.float32
BF16 = mybir.dt.bfloat16
I32 = mybir.dt.int32
U32 = mybir.dt.uint32
U16 = mybir.dt.uint16
U8 = mybir.dt.uint8
FP8X4 = mybir.dt.float8_e4m3fn_x4
FP4X4 = mybir.dt.float4_e2m1fn_x4
ACT = mybir.ActivationFunctionType
ALU = mybir.AluOpType

P = 128
PACK = 4
K_PASS = P * PACK
PASSES = K // K_PASS
LAST = PASSES - 1
TILES = H // P
PAIRS = TILES // 2
BLOCKS = 16
HALF = 512
HALVES = S // HALF
PART = 256
PARTS = S // PART
ROW0 = 32
ROW_BYTES = S + H
SHARED_PASS = 1
LATE_PASS = LAST - 1
AHEAD = 1
SHARE = 128

PLACE_BYTES = 512
PLACES = {
    "picked_scales": 135,
    "w4_raw": 128,
    "tab1": 136,
    "tab0": 96,
    "gain_sb": 96,
    "c_sb": 97,
    "planes1": 98,
    "w1_raw0": 48,
    "w1_raw1": 34,
    "planes2": 60,
    "tab2": 63,
    "w1_raw2": 44,
    "tab3": 4,
    "w1_last0": 64,
    "w1_last1": 72,
    "planes3": 80,
    "wm_raw0": 44,
    "wm_raw1": 52,
    "w1_bf31": 170,
    "wm_bf0": 167,
    "picked_late": 171,
    "wm_bf1": 173,
    "h_bf0": 181,
    "wm_plane1": 181,
    "h_bf256": 182,
    "h_bf512": 189,
    "h_bf768": 190,
    "h_bf896": 188,
}


def tile_list_contrast_metric_distance_kernel(
    tc, tab_words, tab_scales, offs, w1, w4_words, w4_scales, c, gain, wm, out
):
    nc = tc.nc
    with ExitStack() as ctx:
        keep = ctx.enter_context(tc.tile_pool(name="keep", bufs=1))
        reuse = ctx.enter_context(tc.tile_pool(name="reuse", bufs=1))
        psum = ctx.enter_context(tc.psum_pool(name="psum", bufs=1))

        def tile(shape, dtype, name):
            if name in PLACES:
                return reuse.tile(shape, dtype, name=name, align_bytes=256, offset=PLACE_BYTES * PLACES[name])
            return keep.tile(shape, dtype, name=name, align_bytes=256)

        tab = {}
        w1_raw = {}
        w1_last = {}

        def load_tab(a):
            tab[a] = tile([P, T], I32, "tab%d" % a)
            nc.sync.dma_start(tab[a][:], tab_words[a].rearrange("p t i -> p (t i)").bitcast(I32))

        def w1_rows(a):
            return w1[K_PASS * a : K_PASS * (a + 1), :].rearrange("(p i) r -> p i r", i=PACK)

        def load_w1(a):
            w1_raw[a] = tile([P, PACK, H], F32, "w1_raw%d" % a)
            nc.sync.dma_start(w1_raw[a][:], w1_rows(a))

        def load_w1_last():
            rows = w1_rows(LAST)
            for e in range(2):
                w1_last[e] = tile([P, PACK, H // 2], F32, "w1_last%d" % e)
                nc.sync.dma_start(w1_last[e][:], rows[:, :, e * (H // 2) : (e + 1) * (H // 2)])

        offsets = keep.tile([P, S // 16], U16, name="offsets")
        tab_scale_rows = tile([P, T // 4], I32, "tab_scale_rows")
        w4_scale_rows = tile([P, H // 4], I32, "w4_scale_rows")
        row_end = ROW0 + PASSES * BLOCKS
        for raw_rows, scales in ((tab_scale_rows, tab_scales), (w4_scale_rows, w4_scales)):
            nc.vector.memset(raw_rows[0:ROW0, :], 0)
            nc.vector.memset(raw_rows[row_end:P, :], 0)
            nc.sync.dma_start(raw_rows[ROW0:row_end, :], scales.rearrange("a q e -> (a q) e").bitcast(I32))
        nc.sync.dma_start(offsets[:], offs)
        load_tab(0)
        load_w1(0)

        planes = {}

        def clear_planes(a):
            planes[a] = tile([P, ROW_BYTES // 4], I32, "planes%d" % a)
            nc.vector.memset(planes[a][:], 0)

        def move_scale_rows(a):
            first = ROW0 + BLOCKS * a
            for r in range(4):
                nc.sync.dma_start(planes[a][r:P:32, :], scale_rows[first + r : first + BLOCKS : 4, :])

        def plane(a, first, width):
            return planes[a][:].bitcast(U8)[:, first : first + width]

        clear_planes(0)

        banks = [[psum.tile([P, HALF], F32, name="bank%d%d" % (h, t)) for t in range(TILES)] for h in range(HALVES)]
        picked = [[] for a in range(PASSES)]
        w1_bf = [[tile([P, PACK * H // 2], BF16, "w1_bf%d%d" % (a, g)) for g in range(PAIRS)] for a in range(PASSES)]
        w1_codes = [[tile([P, H // 2], U32, "w1_codes%d%d" % (a, g)) for g in range(PAIRS)] for a in range(PASSES)]
        w1_plane = [[tile([P, H // 2], U8, "w1_plane%d%d" % (a, g)) for g in range(PAIRS)] for a in range(PASSES)]

        def gather(a):
            for h in range(HALVES):
                picked[a].append(tile([P, HALF], U32, "picked%d%d" % (a, h)))
                entries = offsets[:, h * (HALF // 16) : (h + 1) * (HALF // 16)]
                nc.vector.tensor_copy(picked[a][h][:], tab[a][:].bitcast(U32).indirect(entries))

        def word_view(a, g):
            return w1_bf[a][g][:].rearrange("p (t m i) -> p m t i", t=2, i=PACK)

        def pair_view(raw, g):
            return raw[:].rearrange("p i (m t) -> p m t i", t=TILES)[:, :, 2 * g : 2 * g + 2, :]

        def round_on_vector(dst, src):
            nc.vector.tensor_scalar(dst, src, -1.0, None, ALU.mult)

        def round_on_scalar(dst, src):
            nc.scalar.activation(dst, src, ACT.Copy, scale=-1.0)

        def w1_prepare(a):
            for g in range(PAIRS):
                round_w1 = round_on_vector if (a, g) == (SHARED_PASS, 0) else round_on_scalar
                round_w1(word_view(a, g), pair_view(w1_raw[a], g))
            for g in range(PAIRS):
                nc.vector.quantize_mx(
                    out=w1_codes[a][g][:].bitcast(FP8X4),
                    scales=w1_plane[a][g][:],
                    in_=w1_bf[a][g][:],
                )

        def w1_last_quantise(t, first, width):
            g, col0 = t // 2, P * (t % 2) + first
            nc.vector.quantize_mx(
                out=w1_codes[LAST][g][:, col0 : col0 + width].bitcast(FP8X4),
                scales=w1_plane[LAST][g][:, col0 : col0 + width],
                in_=w1_bf[LAST][g][:, PACK * col0 : PACK * (col0 + width)],
            )

        def w1_prepare_last():
            half = P // 2
            for e in range(2):
                for g in range(PAIRS):
                    dst, src = word_view(LAST, g)[:, half * e : half * (e + 1)], pair_view(w1_last[e], g)
                    if (e, g) == (1, 0):
                        for t in range(2):
                            round_on_vector(dst[:, :, t, :], src[:, :, t, :])
                    else:
                        round_on_scalar(dst, src)
            for e in range(2):
                for t in range(2):
                    w1_last_quantise(t, e * half, half)
            for t in range(2, TILES):
                w1_last_quantise(t, 0, P)

        def pieces(a, h):
            if (a, h) == (LAST, HALVES - 1):
                return [(picked[a][h], 0, PART), (picked[a][h + 1], PART, PART)]
            return [(picked[a][h], 0, HALF)]

        def pass_w4(a, h, t):
            col0 = (t * PASSES + a) * P
            for words, first, width in pieces(a, h):
                nc.tensor.matmul_mx(
                    out=banks[h][t][:, first : first + width],
                    lhsT=w4_codes[:, col0 // 2 : (col0 + P) // 2].bitcast(FP4X4),
                    lhsT_scale=plane(a, S + t * P, P),
                    rhs=words[:].bitcast(FP8X4),
                    rhs_scale=plane(a, h * HALF + first, width),
                    start=False,
                    stop=False,
                )

        def pass_w1(a, h, t):
            for words, first, width in pieces(a, h):
                nc.tensor.matmul_mx(
                    out=banks[h][t][:, first : first + width],
                    lhsT=w1_codes[a][t // 2][:, P * (t % 2) : P * (t % 2 + 1)].bitcast(FP8X4),
                    lhsT_scale=w1_plane[a][t // 2][:, P * (t % 2) : P * (t % 2 + 1)],
                    rhs=words[:].bitcast(FP8X4),
                    rhs_scale=plane(a, h * HALF + first, width),
                    start=(a == 0),
                    stop=(a == LAST and first + width == HALF),
                )

        def passes(one_pass, a, halves, tiles):
            for h in halves:
                for t in tiles:
                    one_pass(a, h, t)

        both_halves = range(HALVES)
        all_tiles = range(TILES)
        first_pair = range(0, 2)
        second_pair = range(2, TILES)

        scale_rows = tile([P, ROW_BYTES // 4], I32, "scale_rows")
        picked_scales = tile([P, S], U8, "picked_scales")
        nc.vector.tensor_copy(picked_scales[:], tab_scale_rows[:].bitcast(U8).indirect(offsets[:]))
        nc.vector.tensor_copy(
            scale_rows[:].bitcast(U8)[:, S:ROW_BYTES].rearrange("p (t m) -> p t m", t=TILES),
            w4_scale_rows[:].bitcast(U8).rearrange("p (m t) -> p t m", t=TILES),
        )
        nc.vector.tensor_copy(scale_rows[:, 0 : S // 4], picked_scales[:].bitcast(I32))
        move_scale_rows(0)
        w4_raw = tile([P, PASSES * H // 2], I32, "w4_raw")
        nc.sync.dma_start(
            w4_raw[:].rearrange("p (a e) -> p a e", a=PASSES), w4_words.rearrange("a p e -> p a e").bitcast(I32)
        )
        load_tab(1)

        gather(0)
        gain_sb = tile([P, TILES], F32, "gain_sb")
        nc.sync.dma_start(gain_sb[:], gain.rearrange("(p t) -> p t", t=TILES))
        c_sb = tile([P, TILES], F32, "c_sb")
        nc.sync.dma_start(c_sb[:], c.rearrange("(p t) -> p t", t=TILES))
        clear_planes(1)
        move_scale_rows(1)
        guess = tile([P, TILES], F32, "guess")
        inv = tile([P, TILES], F32, "inv")
        quot = tile([P, TILES], F32, "quot")
        twice = tile([P, TILES], F32, "twice")
        root = tile([P, TILES], F32, "root")
        bias = tile([P, TILES], F32, "bias")
        nc.scalar.activation(guess[:], gain_sb[:], ACT.Sqrt)
        nc.vector.reciprocal(inv[:], guess[:])
        nc.vector.tensor_tensor(quot[:], gain_sb[:], inv[:], ALU.mult)
        nc.vector.tensor_tensor(twice[:], quot[:], guess[:], ALU.add)
        nc.vector.tensor_scalar(root[:], twice[:], 0.5, None, ALU.mult)
        nc.vector.tensor_tensor(bias[:], root[:], c_sb[:], ALU.mult)

        w4_codes = tile([P, PASSES * H // 2], I32, "w4_codes")
        nc.vector.tensor_copy(
            w4_codes[:].bitcast(U16).rearrange("p (t m) -> p t m", t=TILES),
            w4_raw[:].bitcast(U16).rearrange("p (m t) -> p t m", t=TILES),
        )

        for a in range(LAST):
            if a > 0:
                gather(a)
            if a == LATE_PASS:
                load_w1_last()
                clear_planes(LAST)
                move_scale_rows(LAST)
                passes(pass_w4, a, both_halves, first_pair)
            w1_prepare(a)
            if a < LATE_PASS:
                load_w1(a + 1)
                load_tab(a + 2)
            if a == 0:
                clear_planes(LATE_PASS)
                move_scale_rows(LATE_PASS)
            if a == LATE_PASS:
                wm_rows = wm.rearrange("(p t) n -> p t n", t=PACK)
                wm_raw = [tile([P, PACK, N // 2], F32, "wm_raw%d" % g) for g in range(PAIRS)]
                for g in range(PAIRS):
                    nc.sync.dma_start(wm_raw[g][:], wm_rows[:, :, g * (N // 2) : (g + 1) * (N // 2)])
            passes(pass_w1, a, both_halves, all_tiles)
            if a == 0:
                passes(pass_w4, a, both_halves, all_tiles)
            elif a < LATE_PASS:
                passes(pass_w4, a, (0,), all_tiles)
                passes(pass_w4, a, (1,), first_pair)
            else:
                passes(pass_w4, a - 1, (1,), second_pair)
                passes(pass_w4, a, both_halves, second_pair)

        def gather_last(name, first, width):
            picked[LAST].append(tile([P, width], U32, name))
            entries = offsets[:, first // 16 : (first + width) // 16]
            nc.vector.tensor_copy(picked[LAST][-1][:], tab[LAST][:].bitcast(U32).indirect(entries))

        gather_last("picked30", 0, HALF)
        gather_last("picked31", HALF, PART)
        passes(pass_w4, LAST, (0,), range(AHEAD))
        w1_prepare_last()
        gather_last("picked_late", HALF + PART, PART)
        for h in both_halves:
            for t in all_tiles:
                if h > 0 or t >= AHEAD:
                    pass_w4(LAST, h, t)
                pass_w1(LAST, h, t)

        squares = [tile([P, TILES, HALF], BF16, "squares%d" % h) for h in both_halves]
        wm_bf = [tile([P, PACK * N // 2], BF16, "wm_bf%d" % g) for g in range(PAIRS)]
        wm_codes = [tile([P, N // 2], U32, "wm_codes%d" % g) for g in range(PAIRS)]
        wm_plane = {}
        for g in range(PAIRS):
            nc.vector.tensor_copy(
                wm_bf[g][:].rearrange("p (m j t) -> p m t j", j=4, t=PACK),
                wm_raw[g][:].rearrange("p t (m j) -> p m t j", j=4),
            )

        def wm_quantise(g):
            wm_plane[g] = tile([P, N // 2], U8, "wm_plane%d" % g)
            nc.vector.quantize_mx(out=wm_codes[g][:].bitcast(FP8X4), scales=wm_plane[g][:], in_=wm_bf[g][:])

        wm_quantise(0)

        h_codes = [tile([P, PART], U32, "h_codes%d" % j) for j in range(PARTS)]
        h_plane = [tile([P, PART], U8, "h_plane%d" % j) for j in range(PARTS)]
        h_bf = {}
        out_rows = out.rearrange("(u p) j -> p u j", p=P)

        def square(h, t, cols):
            nc.scalar.activation(
                squares[h][:, t, cols],
                banks[h][t][:, cols],
                ACT.Square,
                bias=bias[:, t : t + 1],
                scale=root[:, t : t + 1],
            )

        def h_copy(first, width):
            h_bf[first] = tile([P, PACK * width], BF16, "h_bf%d" % first)
            col0 = first % HALF
            nc.vector.tensor_copy(
                h_bf[first][:].rearrange("p (m i t) -> p m t i", i=4, t=PACK),
                squares[first // HALF][:, :, col0 : col0 + width].rearrange("p t (m i) -> p m t i", i=4),
            )

        def h_quantise(first, width):
            j, col0 = first // PART, first % PART
            nc.vector.quantize_mx(
                out=h_codes[j][:, col0 : col0 + width].bitcast(FP8X4),
                scales=h_plane[j][:, col0 : col0 + width],
                in_=h_bf[first][:],
            )

        def h_in_halves(j):
            for step in (h_copy, h_quantise):
                for first in range(j * PART, (j + 1) * PART, PART // 2):
                    step(first, PART // 2)

        def finish_part(j):
            for g in range(PAIRS):
                acc = psum.tile([P, 2, PART], F32, name="bank%d%d" % (j // 2, 2 * (j % 2) + g))
                for e in range(2):
                    nc.tensor.matmul_mx(
                        out=acc[:, e, :],
                        lhsT=wm_codes[g][:, P * e : P * (e + 1)].bitcast(FP8X4),
                        lhsT_scale=wm_plane[g][:, P * e : P * (e + 1)],
                        rhs=h_codes[j][:].bitcast(FP8X4),
                        rhs_scale=h_plane[j][:],
                        start=True,
                        stop=True,
                    )
                dist = tile([P, 2, PART], F32, "dist%d%d" % (j, g))
                nc.scalar.activation(dist[:], acc[:], ACT.Sqrt)
                queue = nc.scalar if (j, g) == (PARTS - 1, PAIRS - 1) else nc.sync
                queue.dma_start(out_rows[:, 2 * g : 2 * g + 2, j * PART : (j + 1) * PART], dist[:])

        last = TILES - 1
        for t in range(last):
            square(0, t, slice(0, HALF))
        for first in range(0, HALF, PART):
            square(0, last, slice(first, first + PART))
        for t in range(last):
            square(1, t, slice(0, HALF))
        square(1, last, slice(0, HALF - SHARE))
        h_in_halves(0)
        h_copy(PART, PART)
        wm_quantise(1)
        h_quantise(PART, PART)
        shifted = tile([P, SHARE], F32, "shifted")
        h_copy(2 * PART, P)
        nc.vector.tensor_scalar(
            shifted[:], banks[1][last][:, HALF - SHARE : HALF], root[:, last:TILES], bias[:, last:TILES], ALU.mult, ALU.add
        )
        h_copy(2 * PART + P, P)
        h_quantise(2 * PART, P)
        h_quantise(2 * PART + P, P)
        nc.vector.tensor_tensor(squares[1][:, last, HALF - SHARE : HALF], shifted[:], shifted[:], ALU.mult)
        h_in_halves(3)
        for j in range(PARTS):
            finish_part(j)
